import numpy as np, ml_dtypes
CORES = [113,118,241,246]
N = 4
BF = ml_dtypes.bfloat16
def gentries(a):
    return np.ascontiguousarray(a.reshape(8, 16, -1).transpose(0, 2, 1)).reshape(8, -1)
def gtable(e):
    e = np.asarray(e); return np.ascontiguousarray(e.reshape(8, -1, 16).transpose(0, 2, 1)).reshape(128, -1).astype(np.int32)
T, C, R, S, VI = 4096, 1024, 48, 20, 6
def parts(rng):
    book = rng.integers(0, T, (N, 8, 16, C)); mix = rng.choice(np.array([0.2, 0.5, 0.8, 1.0]), (N, 8, 1, 1))
    W = np.minimum((256 * ((1 - mix) * rng.random((N, 8, 1, T)) + mix * rng.random((N, 8, 16, T)))).astype(np.int64), 255)
    wt = rng.integers(0, 256, (N, 8, 16)); sg = rng.integers(0, T, (N, 8, T)); sg[:, ::2] = np.argsort(rng.random((N, 4, T)), axis=-1)
    return book, W, wt, sg, rng.integers(0, C, (N, 8, S, R))
def pack(book, W, wt, sg, km):
    return {"book": np.ascontiguousarray(book.reshape(N, 128, C)).astype(np.int32), "tru": np.ascontiguousarray(W.reshape(N, 128, T)).astype(np.float32).astype(BF),
            "wt": np.ascontiguousarray(wt.reshape(N, 128, 1)).astype(np.int32), "sg0": np.stack([gtable(v) for v in sg]), "km0": np.stack([gtable(v.reshape(8, -1)) for v in km])}
def setup_inputs(rng):
    book, W, wt, sg, km = parts(rng)
    km[:, :, :, 3] = km[:, :, :1, 3]; km[:, :, :, 7] = km[:, :, :, 5]; km[:, :, :, 9] = km[:, :, :, 5]
    return pack(book, W, wt, sg, km)
def setup_inputs_spread(rng):
    book, W, wt, sg, km = parts(rng)
    W = np.minimum((np.exp2(8 * rng.random((N, 8, 1, T))) * rng.random((N, 8, 16, T)) * (rng.random((N, 8, 1, T)) > 0.0625)).astype(np.int64), 255)
    W[:, 1::2] = 255 - W[:, 1::2]; wt = np.minimum(np.exp2(8 * rng.random((N, 8, 16))).astype(np.int64), 255)
    book[:, :, ::2] = np.minimum((T * rng.random((N, 8, 8, C)) ** 3).astype(np.int64), T - 1)
    sg[:, ::3] = np.minimum((T * rng.random((N, 3, T)) ** 2).astype(np.int64), T - 1)
    km = np.minimum((C * rng.random((N, 8, S, R)) ** 2).astype(np.int64), C - 1)
    return pack(book, W, wt, sg, km)
def setup_inputs_ends(rng):
    book, W, wt, sg, km = parts(rng)
    kind = rng.random((N, 8, 1, T)); one = (np.arange(16)[:, None] == rng.integers(0, 16, (N, 8, 1, T))).astype(np.int64)
    bits = 255 * rng.integers(0, 2, (N, 8, 16, T))
    W = np.where(kind < 0.2, 255, np.where(kind < 0.32, 255 - one, np.where(kind < 0.44, 0, np.where(kind < 0.5, one, np.where(kind < 0.75, bits, W)))))
    sg = np.where(rng.random((N, 8, T)) < 0.65, (T - 1) * rng.integers(0, 2, (N, 8, T)), sg); sg[..., 0] = 0; sg[..., T - 1] = T - 1
    kc = rng.random((N, 8, 1, C)); two = (T - 1) * rng.integers(0, 2, (N, 8, 16, C))
    book = np.where(kc < 0.22, T - 1, np.where(kc < 0.33, 0, np.where(kc < 0.58, two, np.where((kc < 0.72) & (rng.random(book.shape) < 0.5), two, book))))
    book[..., 0] = (T - 1) * ((np.arange(16) + rng.integers(0, 2, (N, 8, 1))) % 2); book[..., C - 1] = T - 1
    km = np.where(rng.random(km.shape) < 0.65, (C - 1) * rng.integers(0, 2, km.shape), km)
    wt = 255 * rng.integers(0, 2, (N, 8, 16)); wt[:, :, :5] = rng.integers(0, 256, (N, 8, 5)); wt[:, 0] = 255; wt[:, 7] = 255; wt[:, 4] = 0
    for q in range(N):
        for g in range(8):
            kd = (g + q) % 4
            if q == N - 2 or (q == 0 and kd == 2) or (q == N - 1 and g == 7): kd = 0
            P = np.where(rng.permutation(16) < int(rng.integers(8, 10)), 255, 0)
            W[q, g, :, 0] = (0, 255, 255, 255 - P)[kd]; W[q, g, :, T - 1] = (255, 0, 255, P)[kd]
    km[0, :, 0, :] = 0
    km[N - 2, :, 0, :] = C - 1; km[N - 2, :, S - 1, :] = 0; km[N - 2, :, 1:S - 1, R - 1] = C - 1
    km[N - 1, 7, :, R - 1] = C - 1
    W[N - 1, 7, :, 7] = 255 * (np.arange(16) % 2); sg[N - 1, 7, 1] = 0; sg[N - 1, 7, 2] = 7; sg[N - 1, 7, T - 2] = T - 1
    e = np.full(16, 2); e[2] = T - 2; e[15] = T - 1; e[5] = 1; e[14] = 0; book[N - 1, 7, :, 600] = e
    return pack(book, W, wt, sg, km)
def setup_inputs_corners(rng):
    book, W, wt, sg, km = parts(rng); h = C // 2
    km[:, 0] = rng.integers(0, C, (N, 1, R))
    W[:, 1:3, :, :T // 2] = rng.integers(0, 100, (N, 2, 16, T // 2)); W[:, 1:3, :, T // 2:] = rng.integers(156, 256, (N, 2, 16, T - T // 2)); sg[:, 1:3] = np.arange(T)
    book[:, 1:3, :, :h] = rng.integers(T // 2, T, (N, 2, 16, h)); book[:, 1:3, :, h:] = rng.integers(0, T // 2, (N, 2, 16, C - h))
    km[:, 1] = rng.integers(0, h, (N, 1, R)); km[:, 1, S - 1] = rng.integers(h, C, (N, R))
    km[:, 2, 0] = rng.integers(0, h, (N, R)); km[:, 2, 1:] = rng.integers(h, C, (N, S - 1, R))
    book[:, 3, :, ::2] = rng.integers(0, T, (N, 1, h))
    sg[:, 4] = np.where(np.arange(T) % 2 == 0, 0, T - 1); book[:, 4] = (book[:, 4] // 2) * 2 + np.arange(C) % 2
    for q in range(N):
        m = 9 if q % 2 == 0 else 8
        W[q, 4, :, 0] = np.where(np.arange(16) < m, 10, 200); W[q, 4, :, T - 1] = np.where(np.arange(16) < m, 20, 100)
    wt[:, 5] = 0; wt[:, 7] = 255; wt[:, 6] = 255 * rng.integers(0, 2, (N, 16)); wt[:, 6, :4] = rng.integers(1, 256, (N, 4))
    few = np.concatenate([np.array([0, T - 1, 1, T - 2]), rng.permutation(T - 8)[:20] + 4]); book[:, 6] = few[book[:, 6] % 24]
    book[:, 7, 0] = T - 1; sg[:, 7, T - 1] = T - 1; W[:, 7, :, T - 1] = 255
    return pack(book, W, wt, sg, km)
def aim(rng, w, taken, m):
    V = rng.integers(0, 255, (16, 2048)); u = np.add.reduce(w[:, None] * V, axis=0) & 4095; n = ((u * u >> 5) + 37 * u) & (C - 1)
    v, i = np.unique(n, return_index=True); i = rng.permutation(i[~np.isin(v, taken)])[:m]
    return V[:, i], n[i]
def plant(rng, bk, Wg, s, cols, a, b, zero, top, rest, g):
    for j in range(R):
        kind = (j + g) % 3; one = (np.arange(16) == int(rng.integers(0, 16))).astype(np.int64); p, o = rng.permutation(16)[:2]
        pool = (rest, zero, top)[kind]; col = pool[rng.integers(0, len(pool), 16)]
        if kind == 1: p, o = int(rng.integers(1, 16)), 0
        if kind == 2: p, o = 0, int(rng.integers(1, 16))
        col[p] = a[j]; col[o] = b[j]; bk[:, cols[j]] = col
        Wg[:, s[a[j]]] = one if kind == 1 else 255
        Wg[:, s[b[j]]] = 255 - one if kind == 2 else 0
def setup_inputs_full(rng):
    book, W, wt, sg, km = parts(rng); W = np.clip(W, 1, 254); sg = np.argsort(rng.random((N, 8, T)), axis=-1); wt[:, :, 0] = 255
    for r in range(0, N - 1, 2):
        q = r + 1
        for g in range(8):
            x = rng.permutation(T); a0, b0, a1, b1 = np.array(x[:4 * R]).reshape(4, R)
            z, zero, top, rest = x[4 * R:5 * R + 1], x[5 * R + 1:5 * R + 17], x[5 * R + 17:5 * R + 33], x[5 * R + 33:]
            if g == 3: a1[7] = b0[7]; b1[9] = a0[9]
            if g == 5: a1[5] = a0[0]
            y = rng.permutation(C); O, P, X1, X = int(y[0]), int(y[1]), int(y[2]), y[3:3 + R]
            V0, n0 = aim(rng, wt[r, g], y[:3 + R], R); V1, n1 = aim(rng, wt[q, g], np.concatenate([y[:3], n0]), R + 1)
            for c in (r, q):
                W[c, g][:, sg[c, g][zero]] = 0; W[c, g][:, sg[c, g][top]] = 255
            W[r, g][:, sg[r, g][z[:R]]] = V0; book[r, g][:, X] = z[:R]; book[r, g][:, O] = zero[0]
            plant(rng, book[r, g], W[r, g], sg[r, g], n0, a0, b0, zero, top, rest, g)
            km[r, g, 0] = O; km[r, g, 1] = X
            W[q, g][:, sg[q, g][z]] = V1; book[q, g][:, n0] = z[:R]; book[q, g][:, X1] = z[R]
            book[q, g][:, O] = top[0]; book[q, g][:, P] = zero[0]; book[q, g][:, n1[R]] = top[1]
            plant(rng, book[q, g], W[q, g], sg[q, g], n1, a1, b1, zero, top, rest, g + 1)
            if g == 5: book[q, g][:, n1[0]] = a1[0]
            km[q, g, 0] = P; km[q, g, 1] = X1
    return pack(book, W, wt, sg, km)
def setup_inputs_hush(rng):
    book, W, wt, sg, km = parts(rng); q0 = int(rng.integers(0, N))
    for q in (q0, (q0 + 2) % N):
        for g in range(8):
            x = rng.permutation(T)[:3]; m = rng.permutation(T)[:3]; y = rng.permutation(C)[:3]
            hi = rng.integers(160, 255, 16) if g < 7 else np.where(rng.permutation(16) < 9, 254, 255)
            sg[q, g, x] = m; W[q, g, :, m[0]] = 0; W[q, g, :, m[1]] = 255; W[q, g, :, m[2]] = hi
            book[q, g] = np.where(book[q, g] == x[0], x[1], book[q, g]); book[q, g][:, y] = x
            wt[q, g] = rng.integers(224, 256, 16) if g < 7 else 255
            km[q, g, :, ::2] = y[1]; km[q, g, S - 1, ::2] = y[2]; km[(q - 1) % N, g, 0] = y[0]
    return pack(book, W, wt, sg, km)
def check_inputs(d):
    bad = []
    for k, lo, hi in (("book", 0, T - 1), ("tru", 0, 255), ("wt", 0, 255), ("sg0", 0, T - 1), ("km0", 0, C - 1)):
        v = np.asarray(d[k]).astype(np.float64)
        if not (np.min(v) >= lo and np.max(v) <= hi): bad.append("range of " + k)
        elif np.any(np.floor(v) != v): bad.append("whole numbers in " + k)
    return bad
def reference(book, tru, wt, sg0, km0):
    B = np.ascontiguousarray(book.astype(np.int64).reshape(N, 8, 16, C).transpose(0, 1, 3, 2))
    W = np.ascontiguousarray(tru.astype(np.float32).astype(np.int64).reshape(N, 8, 16, T).transpose(0, 1, 3, 2))
    w = wt.astype(np.int64).reshape(N, 8, 16)
    s = np.stack([gentries(v) for v in sg0]).astype(np.int64)
    K = np.stack([gentries(v) for v in km0]).astype(np.int64).reshape(N, 8, S, R)
    a = np.full((N, 8, S, R), -1, np.int64); b = np.full((N, 8, S, R), -1, np.int64)
    last = np.zeros(N, np.int64); ar = np.arange(R)
    for t in range(VI):
        new = np.zeros(N, np.int64)
        for r in range(N):
            q = (r + t) % N
            for g in range(8):
                Z = W[q, g][s[q, g]]
                y = np.min(Z[B[q, g][K[r, g].reshape(-1)]], axis=1).reshape(S, R, 16)
                con = np.add.reduce((y[1:] < y[:1]).astype(np.int64), axis=2) >= 9
                hit = np.any(con, axis=0); ks = np.where(hit, 1 + np.argmax(con, axis=0), 1 + t)
                u = np.add.reduce(y[ks, ar] * w[q, g], axis=1) & 4095
                n = ((u * u >> 5) + 37 * u + last[q]) & (C - 1)
                e = B[q, g][n]; sc = np.add.reduce(Z[e], axis=2)
                na = e[ar, np.argmax(sc, axis=1)]; nb = e[ar, np.argmin(sc, axis=1)]
                oa = np.where(hit, a[r, g, ks, ar], -1); ob = np.where(hit, b[r, g, ks, ar], -1)
                nm = np.stack([na, nb, oa, ob]); nm = np.where(nm < 0, T, nm)
                own = np.full(T + 1, R, np.int64); np.minimum.at(own, nm, np.broadcast_to(ar, (4, R))); own[T] = R
                ok = (na != nb) & (na != oa) & (na != ob) & (nb != oa) & (nb != ob) & ~np.any(own[nm] < ar, axis=0)
                old = np.array(s[q, g]); i = np.nonzero(ok)[0]; h = np.nonzero(ok & (oa >= 0))[0]
                s[q, g, na[i]] = old[nb[i]]; s[q, g, nb[i]] = old[na[i]]
                s[q, g, oa[h]] = old[ob[h]]; s[q, g, ob[h]] = old[oa[h]]
                K[r, g, ks, ar] = n; a[r, g, ks, ar] = np.where(ok, na, -1); b[r, g, ks, ar] = np.where(ok, nb, -1)
                new[q] += np.add.reduce(hit.astype(np.int64))
        last = new
    return {"yk": np.stack([gtable(v.reshape(8, -1)) for v in K]).astype(np.float32), "ya": np.stack([gtable(v.reshape(8, -1)) for v in a]).astype(np.float32),
            "yb": np.stack([gtable(v.reshape(8, -1)) for v in b]).astype(np.float32), "ys": s.astype(np.float32)}

@@ -1,0 +1,444 @@
+from concourse.bass import DstId, RemoteDMATransfer
+from concourse.mybir import dt, AluOpType, AxisListType, ActivationFunctionType
+
+VI = 6
+PADC = 4288
+S_CH = [224, 192, 160, 96, 48, 16]
+V_CH = [144, 144]
+B1, B2 = float(2 ** 23), float(2 ** 21)
+
+_sb = {
+    "truv": (4096, "bfloat16"), "Z": (PADC, "bfloat16"), "S": (PADC, "float32"), "iot": (4096, "float32"),
+    "booki": (1408, "int32"), "blist": (1024, "uint16"), "sgi": (256, "int32"), "sgl": (256, "uint16"),
+    "kmi": (60, "int32"), "wti": (1, "int32"),
+    "G": (16384, "bfloat16"), "ysc": (16400, "bfloat16"), "rst": (4096, "bfloat16"),
+    "pi": (1, "int32"), "pj": (1, "int32"), "pg": (1, "int32"), "colf": (16, "float32"),
+    "iof": (128, "float32"), "iog": (128, "float32"), "ioj": (192, "float32"),
+    "idf": (128, "float32"), "idb": (128, "bfloat16"), "bof": (128, "float32"), "bob": (128, "bfloat16"),
+    "thr": (128, "bfloat16"), "thf": (128, "float32"), "onb": (128, "bfloat16"), "dm": (192, "float32"),
+    "selc": (96, "float32"), "selt": (96, "float32"), "sel8": (8, "float32"), "cntw": (8, "bfloat16"), "usel": (8, "bfloat16"),
+    "scw": (16, "bfloat16"), "pmx": (192, "bfloat16"), "e0": (128, "float32"), "e1": (128, "float32"), "e8": (128, "bfloat16"),
+    "srst": (256, "float32"), "kd1": (160, "float32"), "padf": (12, "float32"), "sumr": (120, "float32"),
+    "kl": (58, "uint16"), "kl2": (6, "uint16"), "y00": (96, "bfloat16"), "y": (912, "bfloat16"), "lt": (912, "bfloat16"),
+    "xx": (160, "float32"), "d1u": (160, "float32"), "su": (320, "float32"), "xt": (48, "float32"), "selo": (96, "float32"),
+    "uI": (3, "int32"), "uU": (3, "int32"), "uV": (3, "int32"), "uQ": (3, "int32"), "uF": (3, "int32"), "uN": (3, "int32"),
+    "uM": (3, "int32"), "nK": (3, "float32"), "nl": (4, "uint16"), "nl6": (6, "uint16"), "bkl": (48, "uint16"), "bk2": (96, "float32"),
+    "zc": (768, "bfloat16"), "ko": (3, "float32"), "kz": (3, "float32"), "kst": (3, "float32"), "hitb": (3, "bfloat16"),
+    "eqo": (60, "float32"), "pr": (120, "float32"), "osm": (120, "float32"), "owno": (6, "float32"), "ownn": (6, "float32"),
+    "zz": (6, "float32"), "f6": (6, "float32"), "prs": (6, "float32"), "dn": (12, "float32"), "dd": (96, "float32"),
+    "sk": (256, "float32"), "ki": (16, "int32"), "kia": (16, "int32"), "kb": (16, "bfloat16"), "xp": (96, "bfloat16"),
+    "em": (96, "float32"), "mb": (96, "float32"), "nsel": (96, "float32"), "fn": (192, "uint16"),
+    "eqb": (2304, "bfloat16"), "cm": (192, "float32"), "m3": (3, "float32"), "acc": (12, "float32"),
+    "of1": (12, "float32"), "of2": (12, "float32"), "offs": (12, "uint16"), "pl": (12, "uint16"),
+    "zp": (192, "bfloat16"), "sp": (192, "float32"), "neq": (60, "float32"), "ab6": (6, "float32"), "val6": (6, "float32"),
+    "xs": (180, "float32"), "ts3": (180, "float32"), "cc": (1, "float32"), "sf": (180, "float32"),
+}
+SCRATCH = {}
+for _k in _sb:
+    SCRATCH[_k] = ("sbuf", [128, _sb[_k][0]], _sb[_k][1])
+for _t in range(VI + 1):
+    SCRATCH["st%d" % _t] = ("sbuf", [128, 180], "float32")
+for _t in range(VI - 1):
+    SCRATCH["so%d" % _t] = ("sbuf", [128, 180], "float32")
+for _t in range(8):
+    SCRATCH["ps%d" % _t] = ("psum", [128, 512], "float32")
+SEMAPHORES = ["sv", "ss", "sp_", "sg_", "lsg", "ltr", "lbk", "lbw", "lkm", "lwt", "dout", "lsem"] + ["arr%d" % _t for _t in range(1, VI + 1)]
+
+
+def rank_program(g, core, T, topo):
+    rank = T.rank_of(core)
+    if rank is None:
+        return
+    A, AX, AF = AluOpType, AxisListType, ActivationFunctionType
+    cores = T.cores
+    nxt, prv = cores[(rank + 1) % 4], cores[(rank + 3) % 4]
+
+    eng = {"v": g.vector, "s": g.scalar, "p": g.tensor, "g": g, "y": g.sync}
+    semn = {"v": "sv", "s": "ss", "p": "sp_", "g": "sg_"}
+    cnt = {"v": 0, "s": 0, "p": 0, "g": 0}
+    waited = {}
+    wr, rd = {}, {}
+
+    def need(q, sem, n):
+        if waited.get((q, sem), 0) < n:
+            waited[(q, sem)] = n
+            eng[q].wait_ge(T.sem[sem], n)
+
+    def deps(q, r, w):
+        lst = {}
+        for k in r:
+            if k in wr:
+                sem, n, q2 = wr[k]
+                if not (q == "p" and q2 == "p"):
+                    lst[sem] = max(lst.get(sem, 0), n)
+        for k in w:
+            if k in wr and wr[k][2] != q:
+                lst[wr[k][0]] = max(lst.get(wr[k][0], 0), wr[k][1])
+            for (sem, n, q2) in rd.get(k, {}).values():
+                if q2 != q:
+                    lst[sem] = max(lst.get(sem, 0), n)
+        for sem in lst:
+            need(q, sem, lst[sem])
+
+    def note(q, r, w, tag):
+        for k in r:
+            rd.setdefault(k, {})[q] = tag
+        for k in w:
+            wr[k] = tag
+            rd[k] = {}
+
+    def E(q, f, r, w):
+        deps(q, r, w)
+        i = f(eng[q])
+        cnt[q] += 1
+        i.then_inc(T.sem[semn[q]], 1)
+        note(q, r, w, (semn[q], cnt[q], q))
+
+    def dma(q, out, in_, sem, r, w):
+        deps(q, r, w)
+        eng[q].dma_start(out=out, in_=in_).then_inc(T.sem[sem], 16)
+        note(q, r, w, (sem, 16, "dma"))
+
+    def ts(out, in0, s1, op0, r, w, s2=None, op1=None):
+        if op1 is None:
+            E("v", lambda e: e.tensor_scalar(out=out, in0=in0, scalar1=s1, scalar2=None, op0=op0), r, w)
+        else:
+            E("v", lambda e: e.tensor_scalar(out=out, in0=in0, scalar1=s1, scalar2=s2, op0=op0, op1=op1), r, w)
+
+    def tt(out, a, b, op, r, w):
+        E("v", lambda e: e.tensor_tensor(out=out, in0=a, in1=b, op=op), r, w)
+
+    def cp(out, a, r, w):
+        E("v", lambda e: e.tensor_copy(out=out, in_=a), r, w)
+
+    def scan(out, d0, d1, op0, op1, r, w):
+        E("v", lambda e: e.tensor_tensor_scan(out=out, data0=d0, data1=d1, initial=0.0, op0=op0, op1=op1), r, w)
+
+    def red(out, a, op, r, w):
+        E("v", lambda e: e.tensor_reduce(out=out, in_=a, axis=AX.X, op=op), r, w)
+
+    def ms(ap, c, w, r=()):
+        E("v", lambda e: e.memset(ap, c), r, w)
+
+    def act(out, a, r, w, **kw):
+        E("s", lambda e: e.activation(out=out, in_=a, func=AF.Copy, **kw), r, w)
+
+    def mm(out, lhsT, rhs, r, w, start=True, stop=True):
+        E("p", lambda e: e.matmul(out, lhsT, rhs, start, stop), r, w)
+
+    def iota(out, pattern, base, cm, w):
+        E("g", lambda e: e.iota(out, pattern, base, cm, allow_small_or_imprecise_dtypes=True), [], w)
+
+    dma("y", T.sgi[:, :], T.sg0[:, :], "lsg", [], ["sgi"])
+    dma("y", T.truv[:, :], T.tru[:, :], "ltr", [], ["truv"])
+    dma("s", T.booki[:, 0:1024], T.book[:, :], "lbk", [], ["bookA"])
+    dma("s", T.kmi[:, :], T.km0[:, :], "lkm", [], ["kmi"])
+    dma("s", T.wti[:, :], T.wt[:, :], "lwt", [], ["wti"])
+    dma("y", T.booki[:, 1024:1408], T.book[:, 0:384], "lbw", [], ["bookB"])
+
+    cp(T.sgl[:, :], T.sgi[:, :], ["sgi"], ["sgl"])
+    ms(T.Z[:, 4096:PADC], 0.0, ["Zpad"])
+    ms(T.rst[:, :], 0.0, ["rst"])
+    ms(T.rst[:, 0:4096:16], 512.0, ["rst"], ["rst"])
+    iota(T.pi[:, :], [[0, 1]], 0, 1, ["pi"])
+    iota(T.iof[:, :], [[1, 128]], 0, 0, ["iof"])
+    iota(T.iog[:, :], [[1, 8], [0, 16]], 0, 0, ["iog"])
+    iota(T.ioj[:, :], [[0, 12], [1, 16]], 0, 0, ["ioj"])
+    iota(T.kd1[:, :], [[0, 8], [1, 20]], 256, 0, ["kd1"])
+    iota(T.padf[:, :], [[16, 12]], 4096, 0, ["padf"])
+    iota(T.iot[:, :], [[1, 4096]], 0, 0, ["iot"])
+    act(T.Z[:, 0:2304], T.truv[:, :].indirect(T.sgl[:, 0:144]), ["truv", "sgl"], ["ZA"])
+    cp(T.blist[:, :], T.booki[:, 0:1024], ["bookA"], ["blist"])
+    cp(T.Z[:, 2304:4096], T.truv[:, :].indirect(T.sgl[:, 144:256]), ["truv", "sgl"], ["ZB"])
+
+    Zk = ["ZA", "ZB", "Zpad"]
+    Zall = T.Z[:, :]
+
+    def yphase(before_tail):
+        pos, items = 0, []
+        for i in range(len(S_CH)):
+            items.append((pos, S_CH[i], "G%d" % i))
+            pos += S_CH[i]
+        vit = []
+        for i in range(len(V_CH)):
+            vit.append((pos, V_CH[i], "H%d" % i))
+            pos += V_CH[i]
+        for (c, n, k) in items:
+            act(T.G[:, 16 * c:16 * (c + n)], Zall.indirect(T.blist[:, c:c + n]), Zk + ["blist"], [k])
+        for (c, n, k) in vit:
+            cp(T.G[:, 16 * c:16 * (c + n)], Zall.indirect(T.blist[:, c:c + n]), Zk + ["blist"], [k])
+        allit = vit + items
+        for i in range(len(allit)):
+            (c, n, k) = allit[i]
+            if i == len(allit) - 2:
+                before_tail()
+            scan(T.ysc[:, 1 + 16 * c:1 + 16 * (c + n)], T.rst[:, 0:16 * n], T.G[:, 16 * c:16 * (c + n)], A.max, A.min, ["rst", k], ["Y"])
+
+    def lists(t):
+        st = T["st%d" % t]
+        sk_ = "st%d" % t
+        ts(T.kl2[:, 0:3], st[:, 0:60:20], 16.0, A.mult, [sk_], ["kl2"])
+        ts(T.kl2[:, 3:6], st[:, 0:60:20], 16.0, A.mult, [sk_], ["kl2"])
+        for jb in range(3):
+            ts(T.kl[:, jb:57:3], st[:, 20 * jb + 1:20 * jb + 20], 16.0, A.mult, [sk_], ["kl"])
+
+    def consts():
+        C = T.colf
+        ts(T.pj[:, :], T.pi[:, :], 15, A.bitwise_and, ["pi"], ["pj"])
+        ts(T.pg[:, :], T.pi[:, :], 4, A.arith_shift_right, ["pi"], ["pg"])
+        cp(C[:, 0:1], T.pi[:, :], ["pi"], ["c0"])
+        cp(C[:, 1:2], T.pj[:, :], ["pj"], ["c1"])
+        cp(C[:, 2:3], T.pg[:, :], ["pg"], ["c2"])
+        cp(C[:, 9:10], T.wti[:, :], ["wti"], ["c9"])
+        ts(C[:, 3:4], C[:, 1:2], 14.5, A.is_lt, ["c1"], ["c3"], B2, A.mult)
+        ts(C[:, 4:5], C[:, 1:2], -1.0, A.mult, ["c1"], ["c4"], 15.0, A.add)
+        ts(C[:, 5:6], C[:, 2:3], 16.0, A.mult, ["c2"], ["c5"], C[:, 0:1], A.add)
+        ts(C[:, 6:7], C[:, 5:6], 16.0, A.add, ["c5"], ["c6"])
+        ts(C[:, 7:8], C[:, 0:1], -8.0, A.add, ["c0"], ["c7"])
+        ts(C[:, 8:9], C[:, 3:4], 276.0, A.add, ["c3"], ["c8"])
+        ts(T.sel8[:, :], T.iof[:, 0:8], C[:, 2:3], A.is_equal, ["iof", "c2"], ["sel8"])
+        ts(T.cntw[:, :], T.sel8[:, :], 32.0, A.mult, ["sel8"], ["cntw"])
+        ts(T.usel[:, :], T.sel8[:, :], C[:, 9:10], A.mult, ["sel8", "c9"], ["usel"])
+        ts(T.scw[:, 0:8], T.sel8[:, :], 16.0, A.mult, ["sel8"], ["scw"])
+        ts(T.scw[:, 8:16], T.sel8[:, :], -16.0, A.mult, ["sel8"], ["scw"])
+        ts(T.idf[:, :], T.iof[:, :], C[:, 0:1], A.is_equal, ["iof", "c0"], ["idf"])
+        ts(T.idb[:, :], T.iof[:, :], C[:, 0:1], A.is_equal, ["iof", "c0"], ["idb"])
+        ts(T.bof[:, :], T.iog[:, :], C[:, 2:3], A.is_equal, ["iog", "c2"], ["bof"])
+        ts(T.bob[:, :], T.iog[:, :], C[:, 2:3], A.is_equal, ["iog", "c2"], ["bob"])
+        ts(T.thf[:, :], T.ioj[:, 0:128], C[:, 1:2], A.is_ge, ["ioj", "c1"], ["thf"])
+        tt(T.thr[:, :], T.thf[:, :], T.bof[:, :], A.mult, ["thf", "bof"], ["thr"])
+        ms(T.onb[:, :], 1.0, ["onb"])
+        ts(T.dm[:, :], T.ioj[:, :], C[:, 1:2], A.is_equal, ["ioj", "c1"], ["dm"])
+        ts(T.selt[:, :], T.ioj[:, 0:96], C[:, 1:2], A.is_le, ["ioj", "c1"], ["selt"], -B1, A.mult)
+        ts(T.selc[:, :], T.ioj[:, 0:96], C[:, 1:2], A.subtract, ["ioj", "c1"], ["selc"], 1.0, A.is_equal)
+        ts(T.selc[:, :], T.selc[:, :], B2, A.mult, ["selc"], ["selc"])
+        tt(T.selc[:, :], T.selc[:, :], T.selt[:, :], A.add, ["selc", "selt"], ["selc"])
+        ts(T.pmx[0:48, 0:96], T.iof[0:48, 0:96], C[0:48, 5:6], A.is_equal, ["iof", "c5"], ["pmx"])
+        ts(T.pmx[0:48, 96:192], T.iof[0:48, 0:96], C[0:48, 6:7], A.is_equal, ["iof", "c6"], ["pmx"])
+        ts(T.e0[0:16, :], T.iog[0:16, :], C[0:16, 0:1], A.is_equal, ["iog", "c0"], ["e0"])
+        ts(T.e1[0:16, :], T.iog[0:16, :], C[0:16, 7:8], A.is_equal, ["iog", "c7"], ["e1"])
+        ts(T.e8[0:8, :], T.iog[0:8, :], C[0:8, 0:1], A.is_equal, ["iog", "c0"], ["e8"])
+        ms(T.srst[:, :], 1.0, ["srst"])
+        ms(T.srst[:, 0:256:16], -1048576.0, ["srst"], ["srst"])
+        ms(T.sumr[:, :], 1.0, ["sumr"])
+        ms(T.sumr[:, 0:120:20], 0.0, ["sumr"], ["sumr"])
+        ts(T.padf[:, :], T.padf[:, :], C[:, 1:2], A.add, ["padf", "c1"], ["padf"])
+        ms(T.S[:, 4096:PADC], 0.0, ["Spad"])
+        ms(T.ps3[:, 0:160], 512.0, ["B3"])
+        ms(T.st0[:, 60:180], 0.0, ["st0n"])
+        for jb in range(3):
+            cp(T.st0[:, 20 * jb:20 * jb + 20], T.kmi[:, jb:60:3], ["kmi"], ["st0"])
+        lists(0)
+
+    def first_tail():
+        consts()
+
+    yphase(first_tail)
+    Sk = ["S0", "S1", "Spad"]
+    C = T.colf
+    ywin = T.ysc[:, 16:16400]
+
+    def sinit(a, b, key):
+        act(T.S[:, a:b], T.iot[:, :].indirect(T.sgl[:, a // 16:b // 16]), ["iot", "sgl"], [key])
+
+    for t in range(VI):
+        st, stk = T["st%d" % t], "st%d" % t
+        last = t == VI - 1
+        M = 2 if t == 0 else 4
+        cp(T.y00[:, :], ywin.indirect(T.kl2[:, 0:6]), ["Y", "kl2"], ["y00"])
+        act(T.y[:, 384:480], ywin.indirect(T.kl[:, 24:30]), ["Y", "kl"], ["yS1"])
+        cp(T.y[:, 0:384], ywin.indirect(T.kl[:, 0:24]), ["Y", "kl"], ["yV"])
+        act(T.y[:, 480:912], ywin.indirect(T.kl[:, 30:57]), ["Y", "kl"], ["yS2"])
+        if t == 0:
+            sinit(0, 2048, "S0")
+        for i in range(5):
+            mm(T.ps0[:, 96 * i:96 * i + 96], T.idb[:, :], T.y00[:, :], ["idb", "y00"], ["B0"])
+        for i in range(5):
+            n = 96 if i < 4 else 48
+            mm(T.ps1[:, 96 * i:96 * i + n], T.idb[:, :], T.y00[:, 0:n], ["idb", "y00"], ["B1"])
+
+        def yslot(k):
+            return T.y[:, 48 * (k - 1):48 * k], ("yV" if k <= 8 else ("yS1" if k <= 10 else "yS2"))
+
+        def usum(k, p):
+            ap, key = yslot(k)
+            mm(T.ps2[0:48, p:160:20], ap, T.usel[:, :], [key, "usel"], ["B2"])
+
+        def csum(k):
+            mm(T.ps3[0:48, 20 - k:160:20], T.lt[:, 48 * (k - 1):48 * k], T.cntw[:, :], ["lt1" if k <= 10 else "lt2", "cntw"], ["B3"])
+
+        usum(1 + t, 0)
+        for k in range(1, 11):
+            usum(k, 20 - k)
+        tt(T.lt[:, 0:480], T.y[:, 0:480], T.ps0[:, 0:480], A.is_lt, ["yV", "yS1", "B0"], ["lt1"])
+        for k in range(1, 11):
+            csum(k)
+        for k in range(11, 20):
+            usum(k, 20 - k)
+        tt(T.lt[:, 480:912], T.y[:, 480:912], T.ps1[:, 0:432], A.is_lt, ["yS2", "B1"], ["lt2"])
+        for k in range(11, 20):
+            csum(k)
+        ts(T.xx[0:48, :], T.ps3[0:48, 0:160], 272.0, A.is_lt, ["B3"], ["xx"], B2, A.mult)
+        scan(T.su[0:48, 160:320], T.ps3[0:48, 0:160], T.kd1[0:48, :], A.max, A.min, ["B3", "kd1"], ["suk"])
+        tt(T.d1u[0:48, :], T.ps2[0:48, 0:160], T.xx[0:48, :], A.subtract, ["B2", "xx"], ["d1u"])
+        scan(T.su[0:48, 0:160], T.xx[0:48, :], T.d1u[0:48, :], A.min, A.max, ["xx", "d1u"], ["suu"])
+        mm(T.ps5[0:16, 0:48], T.su[0:48, 19:320:20], T.idf[0:48, 0:48], ["suk", "suu", "idf"], ["B5"])
+        cp(T.xt[0:16, :], T.ps5[0:16, 0:48], ["B5"], ["xt"])
+        mm(T.ps5[:, 64:112], T.e0[0:16, :], T.xt[0:16, :], ["e0", "xt"], ["B5"])
+        mm(T.ps5[:, 112:160], T.e1[0:16, :], T.xt[0:16, :], ["e1", "xt"], ["B5"])
+        scan(T.selo[:, :], T.selc[:, :], T.ps5[:, 64:160], A.add, A.max, ["selc", "B5"], ["selo"])
+        ts(T.uI[:, :], T.selo[:, 15:48:16], C[:, 3:4], A.subtract, ["selo", "c3"], ["uI"])
+        ts(T.uU[:, :], T.uI[:, :], 4095, A.bitwise_and, ["uI"], ["uU"])
+        ts(T.uV[:, :], T.uU[:, :], 1184.0, A.add, ["uU"], ["uV"])
+        tt(T.uQ[:, :], T.uU[:, :], T.uV[:, :], A.mult, ["uU", "uV"], ["uQ"])
+        ts(T.uF[:, :], T.uQ[:, :], 5, A.arith_shift_right, ["uQ"], ["uF"], 1023, A.bitwise_and)
+        cadd = 0.0 if t == 0 else T.cc[:, 0:1]
+        ck = [] if t == 0 else ["cc"]
+        ts(T.nl[:, 0:3], T.uF[:, :], cadd, A.add, ["uF"] + ck, ["nl"])
+        bwin = T.booki[:, :]
+        cp(T.bkl[:, :], bwin.indirect(T.nl[:, 0:3]), ["bookA", "bookB", "nl"], ["bkl"])
+        act(T.zc[:, 384:768], Zall.indirect(T.bkl[:, 24:48]), Zk + ["bkl"], ["zcS"])
+        cp(T.zc[:, 0:384], Zall.indirect(T.bkl[:, 0:24]), Zk + ["bkl"], ["zcV"])
+        if t == 0:
+            sinit(2048, 4096, "S1")
+        for p in range(16):
+            mm(T.ps4[0:48, p:256:16], T.zc[:, p:768:16], T.scw[:, :], ["zcS", "zcV", "scw"], ["B4"])
+        ts(T.ko[:, :], T.selo[:, 63:96:16], C[:, 8:9], A.subtract, ["selo", "c8"], ["ko"], -1.0, A.mult)
+        if M == 4:
+            for jb in range(3):
+                ts(T.eqo[:, 20 * jb:20 * jb + 20], T.iof[:, 0:20], T.ko[:, jb:jb + 1], A.is_equal, ["iof", "ko"], ["eqo"])
+        ts(T.nl6[:, 0:6:2], T.uF[:, :], cadd, A.add, ["uF"] + ck, ["nl6"])
+        ts(T.nl6[:, 1:6:2], T.uF[:, :], cadd, A.add, ["uF"] + ck, ["nl6"])
+        if M == 4:
+            tt(T.pr[:, 0:60], st[:, 60:120], T.eqo[:, :], A.mult, [stk, "eqo"], ["pr"])
+            tt(T.pr[:, 60:120], st[:, 120:180], T.eqo[:, :], A.mult, [stk, "eqo"], ["pr"])
+        cp(T.bk2[:, :], bwin.indirect(T.nl6[:, :]), ["bookA", "bookB", "nl6"], ["bk2"])
+        if M == 4:
+            scan(T.osm[:, :], T.sumr[:, :], T.pr[:, :], A.mult, A.add, ["sumr", "pr"], ["osm"])
+            ts(T.owno[:, :], T.osm[:, 19:120:20], -1.0, A.add, ["osm"], ["owno"])
+            ts(T.zz[:, :], T.osm[:, 19:120:20], 0.0, A.is_equal, ["osm"], ["zz"], 4097.0, A.mult)
+            tt(T.f6[:, :], T.owno[:, :], T.zz[:, :], A.add, ["owno", "zz"], ["f6"])
+            for jb in range(3):
+                for o in range(2):
+                    c = 32 * jb + 16 * o
+                    E("s", lambda e, c=c, j=3 * o + jb: e.activation(out=T.dd[:, c:c + 16], in_=T.dm[:, 0:16], func=AF.Copy, scale=T.f6[:, j:j + 1]), ["dm", "f6"], ["dd"])
+            mm(T.ps7[:, 0:96], T.bof[:, :], T.dd[:, :], ["bof", "dd"], ["B7"])
+        scan(T.sk[0:48, :], T.srst[0:48, :], T.ps4[0:48, 0:256], A.add, A.max, ["srst", "B4"], ["sk"])
+        cp(T.ki[0:48, :], T.sk[0:48, 15:256:16], ["sk"], ["ki"])
+        ts(T.kia[0:48, :], T.ki[0:48, :], 15, A.bitwise_and, ["ki"], ["kia"])
+        cp(T.kb[0:48, :], T.kia[0:48, :], ["kia"], ["kb"])
+        mm(T.ps6[0:8, 0:96], T.kb[0:48, 0:8], T.pmx[0:48, 0:96], ["kb", "pmx"], ["B6"], True, False)
+        mm(T.ps6[0:8, 0:96], T.kb[0:48, 8:16], T.pmx[0:48, 96:192], ["kb", "pmx"], ["B6"], False, True)
+        if M == 4:
+            for jb in range(3):
+                cp(T.fn[:, 64 * jb + 32:64 * jb + 64], T.ps7[:, 32 * jb:32 * jb + 32], ["B7"], ["fn"])
+        cp(T.xp[0:8, :], T.ps6[0:8, 0:96], ["B6"], ["xp"])
+        mm(T.ps6[:, 96:192], T.e8[0:8, :], T.xp[0:8, :], ["e8", "xp"], ["B6"])
+        ts(T.em[:, :], T.ps6[:, 96:192], C[:, 4:5], A.is_equal, ["B6", "c4"], ["em"])
+        tt(T.mb[:, :], T.em[:, :], T.bk2[:, :], A.mult, ["em", "bk2"], ["mb"])
+        mm(T.ps6[:, 192:288], T.bof[:, :], T.mb[:, :], ["bof", "mb"], ["B6"])
+        if M == 4:
+            ts(T.prs[:, :], T.osm[:, 19:120:20], 0.0, A.is_gt, ["osm"], ["prs"])
+            tt(T.zz[:, :], T.owno[:, :], T.padf[:, 6:12], A.subtract, ["owno", "padf"], ["zz"])
+            tt(T.dn[:, 6:12], T.zz[:, :], T.prs[:, :], A.mult, ["zz", "prs"], ["dnO"])
+        scan(T.nsel[:, :], T.selc[:, :], T.ps6[:, 192:288], A.add, A.max, ["selc", "B6"], ["nsel"])
+        R = 16 * M
+        if M == 2:
+            cp(T.fn[:, 0:96], T.ps6[:, 192:288], ["B6"], ["fn"])
+        else:
+            for jb in range(3):
+                cp(T.fn[:, 64 * jb:64 * jb + 32], T.ps6[:, 192 + 32 * jb:224 + 32 * jb], ["B6"], ["fn"])
+        ts(T.ownn[:, :], T.nsel[:, 15:96:16], C[:, 3:4], A.subtract, ["nsel", "c3"], ["ownn"])
+        tiles = []
+        for jb in range(3):
+            for m in range(M):
+                col = T.ownn[:, 2 * jb + m:2 * jb + m + 1] if m < 2 else T.owno[:, 3 * (m - 2) + jb:3 * (m - 2) + jb + 1]
+                b = 192 * len(tiles)
+                key = "e_%d" % len(tiles)
+                ts(T.eqb[:, b:b + R * (3 - jb)], T.fn[:, R * jb:3 * R], col, A.is_equal, ["fn", "ownn", "owno"] if m >= 2 else ["fn", "ownn"], [key])
+                tiles.append((jb, b, key))
+        for jb in range(3):
+            todo = [(T.bob, "bob", b + R * (jb - j2), key) for (j2, b, key) in tiles if j2 < jb] + [(T.thr, "thr", b, key) for (j2, b, key) in tiles if j2 == jb]
+            for i in range(len(todo)):
+                wm, wk, b, key = todo[i]
+                mm(T.ps7[:, 128 + R * jb:128 + R * jb + R], wm[:, :], T.eqb[:, b:b + R], [wk, key], ["B7"], i == 0, i == len(todo) - 1)
+        LW = 3 * M
+        cp(T.pl[:, 0:6:2], T.ownn[:, 1:6:2], ["ownn"], ["pl"])
+        cp(T.pl[:, 1:6:2], T.ownn[:, 0:6:2], ["ownn"], ["pl"])
+        if M == 4:
+            cp(T.pl[:, 6:9], T.owno[:, 3:6], ["owno"], ["pl"])
+            cp(T.pl[:, 9:12], T.owno[:, 0:3], ["owno"], ["pl"])
+        if not last:
+            act(T.zp[:, 0:16 * LW], Zall.indirect(T.pl[:, 0:LW]), Zk + ["pl"], ["zp"])
+        act(T.sp[:, 0:16 * LW], T.S[:, :].indirect(T.pl[:, 0:LW]), Sk + ["pl"], ["sp"])
+        tt(T.dn[:, 0:6], T.ownn[:, :], T.padf[:, 0:6], A.subtract, ["ownn", "padf"], ["dnN"])
+        tt(T.cm[:, 0:3 * R], T.ps7[:, 128:128 + 3 * R], T.dm[:, 0:3 * R], A.mult, ["B7", "dm"], ["cm"])
+        for jb in range(3):
+            red(T.m3[:, jb:jb + 1], T.cm[:, R * jb:R * jb + R], A.max, ["cm"], ["m3"])
+        for q in range(2):
+            ts(T.acc[:, q:6:2], T.m3[:, :], 1.5, A.is_lt, ["m3"], ["acc"])
+        if M == 4:
+            for o in range(2):
+                ts(T.acc[:, 6 + 3 * o:9 + 3 * o], T.m3[:, :], 1.5, A.is_lt, ["m3"], ["acc"])
+        dk = ["dnN", "dnO"] if M == 4 else ["dnN"]
+        tt(T.of1[:, 0:LW], T.dn[:, 0:LW], T.acc[:, 0:LW], A.mult, dk + ["acc"], ["of1"])
+        tt(T.of2[:, 0:LW], T.of1[:, 0:LW], T.padf[:, 0:LW], A.add, ["of1", "padf"], ["of2"])
+        cp(T.offs[:, 0:LW], T.of2[:, 0:LW], ["of2"], ["offs"])
+        if not last:
+            cp(Zall.indirect(T.offs[:, 0:LW]), T.zp[:, 0:16 * LW], ["offs", "zp"], Zk)
+        ts(T.uN[:, :], T.uF[:, :], cadd, A.add, ["uF"] + ck, ["uN"])
+        ts(T.kz[:, :], T.ko[:, :], 20.0, A.is_equal, ["ko"], ["kz"], float(t + 1 - 20), A.mult)
+        ts(T.val6[:, :], T.ownn[:, :], 1.0, A.add, ["ownn"], ["val6"])
+        ts(T.uM[:, :], T.uN[:, :], 1023, A.bitwise_and, ["uN"], ["uM"])
+        tt(T.kst[:, :], T.kz[:, :], T.ko[:, :], A.add, ["kz", "ko"], ["kst"])
+        tt(T.ab6[:, :], T.val6[:, :], T.acc[:, 0:6], A.mult, ["val6", "acc"], ["ab6"])
+        cp(T.nK[:, :], T.uM[:, :], ["uM"], ["nK"])
+        for jb in range(3):
+            kc = T.kst[:, jb:jb + 1]
+            ts(T.neq[:, 20 * jb:20 * jb + 20], T.iof[:, 0:20], kc, A.not_equal, ["iof", "kst"], ["neq"])
+        for jb in range(3):
+            kc = T.kst[:, jb:jb + 1]
+            for a in range(3):
+                v = T.nK[:, jb:jb + 1] if a == 0 else T.ab6[:, 2 * jb + a - 1:2 * jb + a]
+                c = 60 * a + 20 * jb
+                ts(T.xs[:, c:c + 20], T.iof[:, 0:20], kc, A.is_equal, ["iof", "kst", "nK", "ab6"], ["xs"], v, A.mult)
+        for a in range(3):
+            tt(T.ts3[:, 60 * a:60 * a + 60], st[:, 60 * a:60 * a + 60], T.neq[:, :], A.mult, [stk, "neq"] + (["st0n"] if t == 0 else []), ["ts3"])
+        if not last:
+            sok = "so%d" % t
+            tt(T[sok][:, :], T.ts3[:, :], T.xs[:, :], A.add, ["ts3", "xs"], [sok])
+            dst, src_ap = nxt, T[sok][:, :]
+        else:
+            tt(T.ts3[:, :], T.ts3[:, :], T.xs[:, :], A.add, ["ts3", "xs"], ["ts3"])
+            for a in range(3):
+                for jb in range(3):
+                    o_, i_ = T.sf[:, 60 * a + jb:60 * a + 60:3], T.ts3[:, 60 * a + 20 * jb:60 * a + 20 * jb + 20]
+                    ts(o_, i_, 0.0 if a == 0 else -1.0, A.add, ["ts3"], ["sf"])
+            sok = "sf"
+            dst, src_ap = prv, T.sf[:, :]
+        deps("g", [sok], [])
+        rid, pid = topo.addr(dst, core)
+        en = topo.engines(core, dst)[:8]
+        g.remote_dma(out_ap=T["st%d" % (t + 1)][:, :], in_ap=src_ap, remote_sem=T.sem["arr%d" % (t + 1)], local_sem=T.sem.lsem,
+                     pid=pid, routing_id=rid, dma_engine_mask=sum(1 << e for e in en))
+        cnt["sent"] = cnt.get("sent", 0) + len(en)
+        frm = prv if not last else nxt
+        wr["st%d" % (t + 1)] = ("arr%d" % (t + 1), len(topo.engines(frm, core)[:8]), "remote")
+        cp(T.S[:, :].indirect(T.offs[:, 0:LW]), T.sp[:, 0:16 * LW], ["offs", "sp"], Sk)
+        if last:
+            dma("y", T.ys[:, :], T.S[0:128:16, 0:4096], "dout", Sk, [])
+            break
+        ts(T.hitb[:, :], T.ko[:, :], 19.5, A.is_lt, ["ko"], ["hitb"])
+        mm(T.ps7[:, 384:387], T.onb[:, :], T.hitb[:, :], ["onb", "hitb"], ["B7"])
+        red(T.cc[:, :], T.ps7[:, 384:387], A.add, ["B7"], ["cc"])
+        yphase(lambda t=t: lists(t + 1))
+
+    fin = T["st%d" % VI]
+    k = "st%d" % VI
+    dma("y", T.yk[:, :], fin[:, 0:60], "dout", [k], [])
+    dma("y", T.ya[:, :], fin[:, 60:120], "dout", [k], [])
+    dma("y", T.yb[:, :], fin[:, 120:180], "dout", [k], [])
+    need("y", "dout", 64)
+    need("g", "lsem", cnt["sent"])
+    for q in ("v", "s", "p", "g"):
+        need("g", semn[q], cnt[q])

@@ -3,29 +3,34 @@ from concourse.mybir import dt, AluOpType, AxisListType, ActivationFunctionType
 
 VI = 6
 PADC = 4288
-S_CH = [224, 192, 160, 96, 48, 16]
-V_CH = [144, 144]
+PH = 344
+P_CH = [96, 120, 128]
+S_CH = [128, 104, 68, 28, 8]
+S0_CH = [128, 128, 128, 128, 128, 80, 48, 16]
+V0_CH = [128, 112]
+YW = 1 + 16 * 1024
 B1, B2 = float(2 ** 23), float(2 ** 21)
 
 _sb = {
     "truv": (4096, "bfloat16"), "Z": (PADC, "bfloat16"), "S": (PADC, "float32"), "iot": (4096, "float32"),
-    "booki": (1408, "int32"), "blist": (1024, "uint16"), "sgi": (256, "int32"), "sgl": (256, "uint16"),
-    "kmi": (60, "int32"), "wti": (1, "int32"),
-    "G": (16384, "bfloat16"), "ysc": (16400, "bfloat16"), "rst": (4096, "bfloat16"),
+    "booki": (1408, "int32"), "blist": (1024 - 2 * PH, "uint16"), "sgi": (256, "int32"), "sgl": (256, "uint16"),
+    "kmi": (64, "int32"),
+    "G": (16384, "bfloat16"), "blist0": (1024, "uint16"), "H": (16 * PH, "bfloat16"), "ysc": (YW, "bfloat16"), "rst": (2048, "bfloat16"), "rst8": (2048, "bfloat16"),
+    "lai": (PH, "int32"), "lbi": (PH, "int32"), "la": (PH, "uint16"), "lb": (PH, "uint16"),
+    "lzz": (240, "float32"), "pad8": (24, "float32"),
     "pi": (1, "int32"), "pj": (1, "int32"), "pg": (1, "int32"), "colf": (16, "float32"),
     "iof": (128, "float32"), "iog": (128, "float32"), "ioj": (192, "float32"),
     "idf": (128, "float32"), "idb": (128, "bfloat16"), "bof": (128, "float32"), "bob": (128, "bfloat16"),
     "thr": (128, "bfloat16"), "thf": (128, "float32"), "onb": (128, "bfloat16"), "dm": (192, "float32"),
-    "selc": (96, "float32"), "selt": (96, "float32"), "sel8": (8, "float32"), "cntw": (8, "bfloat16"), "usel": (8, "bfloat16"),
+    "selc": (96, "float32"), "selt": (96, "float32"), "selc2": (96, "float32"), "sel8": (8, "float32"), "cntw": (8, "bfloat16"), "usel": (8, "bfloat16"),
     "scw": (16, "bfloat16"), "pmx": (192, "bfloat16"), "e0": (128, "float32"), "e1": (128, "float32"), "e8": (128, "bfloat16"),
     "srst": (256, "float32"), "kd1": (160, "float32"), "padf": (12, "float32"), "sumr": (120, "float32"),
     "kl": (58, "uint16"), "kl2": (6, "uint16"), "y00": (96, "bfloat16"), "y": (912, "bfloat16"), "lt": (912, "bfloat16"),
     "xx": (160, "float32"), "d1u": (160, "float32"), "su": (320, "float32"), "xt": (48, "float32"), "selo": (96, "float32"),
-    "uI": (3, "int32"), "uU": (3, "int32"), "uV": (3, "int32"), "uQ": (3, "int32"), "uF": (3, "int32"), "uN": (3, "int32"),
-    "uM": (3, "int32"), "nK": (3, "float32"), "nl": (4, "uint16"), "nl6": (6, "uint16"), "bkl": (48, "uint16"), "bk2": (96, "float32"),
+    "uint": (28, "int32"), "nK": (3, "float32"), "nl": (4, "uint16"), "nl6": (6, "uint16"), "bkl": (48, "uint16"), "bk2": (96, "float32"),
     "zc": (768, "bfloat16"), "ko": (3, "float32"), "kz": (3, "float32"), "kst": (3, "float32"), "hitb": (3, "bfloat16"),
-    "eqo": (60, "float32"), "pr": (120, "float32"), "osm": (120, "float32"), "owno": (6, "float32"), "ownn": (6, "float32"),
-    "zz": (6, "float32"), "f6": (6, "float32"), "prs": (6, "float32"), "dn": (12, "float32"), "dd": (96, "float32"),
+    "eqo": (60, "float32"), "pr": (120, "float32"), "osm": (120, "float32"), "owno": (6, "float32"), "owno2": (6, "float32"), "ownn": (6, "float32"),
+    "zz": (6, "float32"), "f6": (6, "float32"), "dn": (12, "float32"), "dd": (96, "float32"),
     "sk": (256, "float32"), "ki": (16, "int32"), "kia": (16, "int32"), "kb": (16, "bfloat16"), "xp": (96, "bfloat16"),
     "em": (96, "float32"), "mb": (96, "float32"), "nsel": (96, "float32"), "fn": (192, "uint16"),
     "eqb": (2304, "bfloat16"), "cm": (192, "float32"), "m3": (3, "float32"), "acc": (12, "float32"),
@@ -42,7 +47,7 @@ for _t in range(VI - 1):
     SCRATCH["so%d" % _t] = ("sbuf", [128, 180], "float32")
 for _t in range(8):
     SCRATCH["ps%d" % _t] = ("psum", [128, 512], "float32")
-SEMAPHORES = ["sv", "ss", "sp_", "sg_", "lsg", "ltr", "lbk", "lbw", "lkm", "lwt", "dout", "lsem"] + ["arr%d" % _t for _t in range(1, VI + 1)]
+SEMAPHORES = ["sv", "ss", "sp_", "sg_", "lsg", "ltr", "lbk", "lbw", "lkm", "lwt", "lhf", "lhg", "dout", "lsem"] + ["arr%d" % _t for _t in range(1, VI + 1)]
 
 
 def rank_program(g, core, T, topo):
@@ -75,7 +80,7 @@ def rank_program(g, core, T, topo):
             if k in wr and wr[k][2] != q:
                 lst[wr[k][0]] = max(lst.get(wr[k][0], 0), wr[k][1])
             for (sem, n, q2) in rd.get(k, {}).values():
-                if q2 != q:
+                if q2 != q or q == "v":
                     lst[sem] = max(lst.get(sem, 0), n)
         for sem in lst:
             need(q, sem, lst[sem])
@@ -132,14 +137,25 @@ def rank_program(g, core, T, topo):
     dma("y", T.sgi[:, :], T.sg0[:, :], "lsg", [], ["sgi"])
     dma("y", T.truv[:, :], T.tru[:, :], "ltr", [], ["truv"])
     dma("s", T.booki[:, 0:1024], T.book[:, :], "lbk", [], ["bookA"])
-    dma("s", T.kmi[:, :], T.km0[:, :], "lkm", [], ["kmi"])
-    dma("s", T.wti[:, :], T.wt[:, :], "lwt", [], ["wti"])
+    dma("y", T.kmi[:, 60:61], T.wt[:, :], "lwt", [], ["wti"])
+    dma("y", T.kmi[:, 0:60], T.km0[:, :], "lkm", [], ["kmi"])
     dma("y", T.booki[:, 1024:1408], T.book[:, 0:384], "lbw", [], ["bookB"])
+
+    def halves(q, buf, o, key, sem):
+        for p in range(8):
+            for h in range(2):
+                eng[q].dma_start(out=buf[p + 8 * h:128:16, :], in_=T.book[p + o:128:16, 512 * h:512 * h + PH]).then_inc(T.sem[sem], 16)
+        note(q, [], [key], (sem, 256, "dma"))
+
+    halves("y", T.lbi, 8, "lbi", "lhf")
 
     cp(T.sgl[:, :], T.sgi[:, :], ["sgi"], ["sgl"])
     ms(T.Z[:, 4096:PADC], 0.0, ["Zpad"])
     ms(T.rst[:, :], 0.0, ["rst"])
-    ms(T.rst[:, 0:4096:16], 512.0, ["rst"], ["rst"])
+    ms(T.rst8[:, :], 0.0, ["rst8"])
+    ms(T.rst[:, 0:2048:16], 512.0, ["rst"], ["rst"])
+    ms(T.rst8[:, 0:2048:8], 512.0, ["rst8"], ["rst8"])
+    ms(T.ysc[:, 0:1], 0.0, ["Y0"])
     iota(T.pi[:, :], [[0, 1]], 0, 1, ["pi"])
     iota(T.iof[:, :], [[1, 128]], 0, 0, ["iof"])
     iota(T.iog[:, :], [[1, 8], [0, 16]], 0, 0, ["iog"])
@@ -147,40 +163,50 @@ def rank_program(g, core, T, topo):
     iota(T.kd1[:, :], [[0, 8], [1, 20]], 256, 0, ["kd1"])
     iota(T.padf[:, :], [[16, 12]], 4096, 0, ["padf"])
     iota(T.iot[:, :], [[1, 4096]], 0, 0, ["iot"])
-    act(T.Z[:, 0:2304], T.truv[:, :].indirect(T.sgl[:, 0:144]), ["truv", "sgl"], ["ZA"])
-    cp(T.blist[:, :], T.booki[:, 0:1024], ["bookA"], ["blist"])
-    cp(T.Z[:, 2304:4096], T.truv[:, :].indirect(T.sgl[:, 144:256]), ["truv", "sgl"], ["ZB"])
-
+    halves("g", T.lai, 0, "lai", "lhg")
+    act(T.Z[:, 0:2048], T.truv[:, :].indirect(T.sgl[:, 0:128]), ["truv", "sgl"], ["ZA"])
     Zk = ["ZA", "ZB", "Zpad"]
     Zall = T.Z[:, :]
 
     def yphase(before_tail):
-        pos, items = 0, []
+        c, pits, sits = 0, [], []
+        for i in range(len(P_CH)):
+            pits.append((c, P_CH[i], "G%d" % i, "H%d" % i))
+            c += P_CH[i]
         for i in range(len(S_CH)):
-            items.append((pos, S_CH[i], "G%d" % i))
-            pos += S_CH[i]
-        vit = []
-        for i in range(len(V_CH)):
-            vit.append((pos, V_CH[i], "H%d" % i))
-            pos += V_CH[i]
-        for (c, n, k) in items:
-            act(T.G[:, 16 * c:16 * (c + n)], Zall.indirect(T.blist[:, c:c + n]), Zk + ["blist"], [k])
-        for (c, n, k) in vit:
-            cp(T.G[:, 16 * c:16 * (c + n)], Zall.indirect(T.blist[:, c:c + n]), Zk + ["blist"], [k])
-        allit = vit + items
-        for i in range(len(allit)):
-            (c, n, k) = allit[i]
-            if i == len(allit) - 2:
-                before_tail()
+            sits.append((c, S_CH[i], "J%d" % i))
+            c += S_CH[i]
+        for (c, n, k, k2) in pits:
+            act(T.G[:, 16 * c:16 * (c + n)], Zall.indirect(T.lb[:, c:c + n]), Zk + ["lb"], [k])
+        for (c, n, k) in sits:
+            act(T.G[:, 16 * c:16 * (c + n)], Zall.indirect(T.blist[:, c - PH:c - PH + n]), Zk + ["blist"], [k])
+        for (c, n, k, k2) in pits:
+            tt(T.H[:, 16 * c:16 * (c + n)], Zall.indirect(T.la[:, c:c + n]), T.G[:, 16 * c:16 * (c + n)], A.min, Zk + ["la", k], [k2])
+        for (c, n, k, k2) in pits:
+            scan(T.ysc[:, 1 + 16 * c:1 + 16 * (c + n)], T.rst8[:, 0:16 * n], T.H[:, 16 * c:16 * (c + n)], A.max, A.min, ["rst8", k2], ["Y"])
+        for i in range(len(sits)):
+            (c, n, k) = sits[i]
+            before_tail(i)
             scan(T.ysc[:, 1 + 16 * c:1 + 16 * (c + n)], T.rst[:, 0:16 * n], T.G[:, 16 * c:16 * (c + n)], A.max, A.min, ["rst", k], ["Y"])
 
-    def lists(t):
+    def lists(t, i):
         st = T["st%d" % t]
         sk_ = "st%d" % t
-        ts(T.kl2[:, 0:3], st[:, 0:60:20], 16.0, A.mult, [sk_], ["kl2"])
-        ts(T.kl2[:, 3:6], st[:, 0:60:20], 16.0, A.mult, [sk_], ["kl2"])
+        lz, lz2, lw = T.lzz[:, 0:60], T.lzz[:, 60:120], T.lzz[:, 120:180]
+        if i == 0:
+            ts(lz, st[:, 0:60], 511.5, A.is_ge, [sk_], ["lz"], -511.5, A.mult)
+        if i == 1:
+            tt(lz2, st[:, 0:60], lz, A.add, [sk_, "lz"], ["lz2"])
+        if i == 2:
+            ts(lw, lz2, -(PH - 0.5), A.add, ["lz2"], ["lw"], 0.0, A.max)
+        if i == 3:
+            tt(T.lzz[:, 180:240], lz2, lw, A.add, ["lz2", "lw"], ["lz3"])
+        if i < 4:
+            return
+        ts(T.kl2[:, 0:3], T.lzz[:, 180:240:20], 16.0, A.mult, ["lz3"], ["kl2"], 8.0, A.add)
+        ts(T.kl2[:, 3:6], T.lzz[:, 180:240:20], 16.0, A.mult, ["lz3"], ["kl2"], 8.0, A.add)
         for jb in range(3):
-            ts(T.kl[:, jb:57:3], st[:, 20 * jb + 1:20 * jb + 20], 16.0, A.mult, [sk_], ["kl"])
+            ts(T.kl[:, jb:57:3], T.lzz[:, 181 + 20 * jb:200 + 20 * jb], 16.0, A.mult, ["lz3"], ["kl"], 8.0, A.add)
 
     def consts():
         C = T.colf
@@ -189,7 +215,7 @@ def rank_program(g, core, T, topo):
         cp(C[:, 0:1], T.pi[:, :], ["pi"], ["c0"])
         cp(C[:, 1:2], T.pj[:, :], ["pj"], ["c1"])
         cp(C[:, 2:3], T.pg[:, :], ["pg"], ["c2"])
-        cp(C[:, 9:10], T.wti[:, :], ["wti"], ["c9"])
+        cp(C[:, 9:10], T.kmi[:, 60:61], ["wti"], ["c9"])
         ts(C[:, 3:4], C[:, 1:2], 14.5, A.is_lt, ["c1"], ["c3"], B2, A.mult)
         ts(C[:, 4:5], C[:, 1:2], -1.0, A.mult, ["c1"], ["c4"], 15.0, A.add)
         ts(C[:, 5:6], C[:, 2:3], 16.0, A.mult, ["c2"], ["c5"], C[:, 0:1], A.add)
@@ -204,8 +230,8 @@ def rank_program(g, core, T, topo):
         ts(T.idf[:, :], T.iof[:, :], C[:, 0:1], A.is_equal, ["iof", "c0"], ["idf"])
         ts(T.idb[:, :], T.iof[:, :], C[:, 0:1], A.is_equal, ["iof", "c0"], ["idb"])
         ts(T.bof[:, :], T.iog[:, :], C[:, 2:3], A.is_equal, ["iog", "c2"], ["bof"])
-        ts(T.bob[:, :], T.iog[:, :], C[:, 2:3], A.is_equal, ["iog", "c2"], ["bob"])
-        ts(T.thf[:, :], T.ioj[:, 0:128], C[:, 1:2], A.is_ge, ["ioj", "c1"], ["thf"])
+        ts(T.bob[:, :], T.iog[:, :], C[:, 2:3], A.is_equal, ["iog", "c2"], ["bob"], 8192.0, A.mult)
+        ts(T.thf[:, :], T.ioj[:, 0:128], C[:, 1:2], A.is_ge, ["ioj", "c1"], ["thf"], 8192.0, A.mult)
         tt(T.thr[:, :], T.thf[:, :], T.bof[:, :], A.mult, ["thf", "bof"], ["thr"])
         ms(T.onb[:, :], 1.0, ["onb"])
         ts(T.dm[:, :], T.ioj[:, :], C[:, 1:2], A.is_equal, ["ioj", "c1"], ["dm"])
@@ -213,6 +239,11 @@ def rank_program(g, core, T, topo):
         ts(T.selc[:, :], T.ioj[:, 0:96], C[:, 1:2], A.subtract, ["ioj", "c1"], ["selc"], 1.0, A.is_equal)
         ts(T.selc[:, :], T.selc[:, :], B2, A.mult, ["selc"], ["selc"])
         tt(T.selc[:, :], T.selc[:, :], T.selt[:, :], A.add, ["selc", "selt"], ["selc"])
+        ts(C[:, 10:11], C[:, 1:2], 14.5, A.is_lt, ["c1"], ["c10"], 8192.0, A.mult)
+        ts(T.selt[:, :], T.ioj[:, 0:96], C[:, 1:2], A.is_le, ["ioj", "c1"], ["selt"], -131072.0, A.mult)
+        ts(T.selc2[:, :], T.ioj[:, 0:96], C[:, 1:2], A.subtract, ["ioj", "c1"], ["selc2"], 1.0, A.is_equal)
+        ts(T.selc2[:, :], T.selc2[:, :], 8192.0, A.mult, ["selc2"], ["selc2"])
+        tt(T.selc2[:, :], T.selc2[:, :], T.selt[:, :], A.add, ["selc2", "selt"], ["selc2"])
         ts(T.pmx[0:48, 0:96], T.iof[0:48, 0:96], C[0:48, 5:6], A.is_equal, ["iof", "c5"], ["pmx"])
         ts(T.pmx[0:48, 96:192], T.iof[0:48, 0:96], C[0:48, 6:7], A.is_equal, ["iof", "c6"], ["pmx"])
         ts(T.e0[0:16, :], T.iog[0:16, :], C[0:16, 0:1], A.is_equal, ["iog", "c0"], ["e0"])
@@ -222,21 +253,36 @@ def rank_program(g, core, T, topo):
         ms(T.srst[:, 0:256:16], -1048576.0, ["srst"], ["srst"])
         ms(T.sumr[:, :], 1.0, ["sumr"])
         ms(T.sumr[:, 0:120:20], 0.0, ["sumr"], ["sumr"])
-        ts(T.padf[:, :], T.padf[:, :], C[:, 1:2], A.add, ["padf", "c1"], ["padf"])
+        ts(T.pad8[:, 0:12], T.padf[:, :], C[:, 1:2], A.add, ["padf", "c1"], ["pad8"])
+        ts(T.pad8[:, 12:24], T.padf[:, :], C[:, 1:2], A.add, ["padf", "c1"], ["pad8"], 8192.0, A.add)
         ms(T.S[:, 4096:PADC], 0.0, ["Spad"])
         ms(T.ps3[:, 0:160], 512.0, ["B3"])
         ms(T.st0[:, 60:180], 0.0, ["st0n"])
         for jb in range(3):
             cp(T.st0[:, 20 * jb:20 * jb + 20], T.kmi[:, jb:60:3], ["kmi"], ["st0"])
-        lists(0)
 
-    def first_tail():
-        consts()
-
-    yphase(first_tail)
+    cp(T.blist0[:, :], T.booki[:, 0:1024], ["bookA"], ["blist0"])
+    cp(T.Z[:, 2048:4096], T.truv[:, :].indirect(T.sgl[:, 128:256]), ["truv", "sgl"], ["ZB"])
+    c, its = 0, []
+    for (chs, nm) in ((S0_CH, "J"), (V0_CH, "V")):
+        for i in range(len(chs)):
+            its.append((c, chs[i], nm + "0%d" % i, nm))
+            c += chs[i]
+    for (c, n, k, nm) in its:
+        (act if nm == "J" else cp)(T.G[:, 16 * c:16 * (c + n)], Zall.indirect(T.blist0[:, c:c + n]), Zk + ["blist0"], [k])
+    consts()
+    for jb in range(3):
+        ts(T.kl[:, jb:57:3], T.st0[:, 20 * jb + 1:20 * jb + 20], 16.0, A.mult, ["st0"], ["kl"], 16.0, A.add)
+    for i in range(2):
+        ts(T.kl2[:, 3 * i:3 * i + 3], T.st0[:, 0:60:20], 16.0, A.mult, ["st0"], ["kl2"], 16.0, A.add)
+    for (c, n, k, nm) in its[len(S0_CH):] + its[:len(S0_CH)]:
+        scan(T.ysc[:, 1 + 16 * c:1 + 16 * (c + n)], T.rst[:, 0:16 * n], T.G[:, 16 * c:16 * (c + n)], A.max, A.min, ["rst", k], ["Y"])
+    for k in ("J", "V"):
+        for i in range(8):
+            wr.pop(k + "0%d" % i, None)
     Sk = ["S0", "S1", "Spad"]
     C = T.colf
-    ywin = T.ysc[:, 16:16400]
+    ywin = T.ysc[:, :]
 
     def sinit(a, b, key):
         act(T.S[:, a:b], T.iot[:, :].indirect(T.sgl[:, a // 16:b // 16]), ["iot", "sgl"], [key])
@@ -273,11 +319,13 @@ def rank_program(g, core, T, topo):
         tt(T.lt[:, 0:480], T.y[:, 0:480], T.ps0[:, 0:480], A.is_lt, ["yV", "yS1", "B0"], ["lt1"])
         for k in range(1, 11):
             csum(k)
-        for k in range(11, 20):
-            usum(k, 20 - k)
         tt(T.lt[:, 480:912], T.y[:, 480:912], T.ps1[:, 0:432], A.is_lt, ["yS2", "B1"], ["lt2"])
         for k in range(11, 20):
             csum(k)
+        for k in range(11, 20):
+            usum(k, 20 - k)
+        if t == 0:
+            cp(T.lb[:, :], T.lbi[:, :], ["lbi"], ["lb"])
         ts(T.xx[0:48, :], T.ps3[0:48, 0:160], 272.0, A.is_lt, ["B3"], ["xx"], B2, A.mult)
         scan(T.su[0:48, 160:320], T.ps3[0:48, 0:160], T.kd1[0:48, :], A.max, A.min, ["B3", "kd1"], ["suk"])
         tt(T.d1u[0:48, :], T.ps2[0:48, 0:160], T.xx[0:48, :], A.subtract, ["B2", "xx"], ["d1u"])
@@ -287,133 +335,164 @@ def rank_program(g, core, T, topo):
         mm(T.ps5[:, 64:112], T.e0[0:16, :], T.xt[0:16, :], ["e0", "xt"], ["B5"])
         mm(T.ps5[:, 112:160], T.e1[0:16, :], T.xt[0:16, :], ["e1", "xt"], ["B5"])
         scan(T.selo[:, :], T.selc[:, :], T.ps5[:, 64:160], A.add, A.max, ["selc", "B5"], ["selo"])
-        ts(T.uI[:, :], T.selo[:, 15:48:16], C[:, 3:4], A.subtract, ["selo", "c3"], ["uI"])
-        ts(T.uU[:, :], T.uI[:, :], 4095, A.bitwise_and, ["uI"], ["uU"])
-        ts(T.uV[:, :], T.uU[:, :], 1184.0, A.add, ["uU"], ["uV"])
-        tt(T.uQ[:, :], T.uU[:, :], T.uV[:, :], A.mult, ["uU", "uV"], ["uQ"])
-        ts(T.uF[:, :], T.uQ[:, :], 5, A.arith_shift_right, ["uQ"], ["uF"], 1023, A.bitwise_and)
+        uI, uU, uV, uQ, uF, uN, uM = [T.uint[:, 4 * i:4 * i + 3] for i in range(7)]
+        def eqold(jb):
+            if M == 4:
+                ts(T.eqo[:, 20 * jb:20 * jb + 20], T.iof[:, 0:20], T.ko[:, jb:jb + 1], A.is_equal, ["iof", "ko"], ["eqo"])
+
+        def prold(a):
+            if M == 4:
+                tt(T.pr[:, 60 * a - 60:60 * a], st[:, 60 * a:60 * a + 60], T.eqo[:, :], A.mult, [stk, "eqo"], ["pr"])
+
+        cp(uI, T.selo[:, 15:48:16], ["selo"], ["uI"])
+        ts(T.ko[:, :], T.selo[:, 63:96:16], C[:, 8:9], A.subtract, ["selo", "c8"], ["ko"], -1.0, A.mult)
+        ts(uU, uI, 4095, A.bitwise_and, ["uI"], ["uU"])
+        eqold(0)
+        eqold(1)
+        ts(uV, uU, 1184.0, A.add, ["uU"], ["uV"])
+        eqold(2)
+        tt(uQ, uU, uV, A.mult, ["uU", "uV"], ["uQ"])
+        prold(1)
+        ts(uF, uQ, 5, A.arith_shift_right, ["uQ"], ["uF"], 1023, A.bitwise_and)
+        prold(2)
         cadd = 0.0 if t == 0 else T.cc[:, 0:1]
         ck = [] if t == 0 else ["cc"]
-        ts(T.nl[:, 0:3], T.uF[:, :], cadd, A.add, ["uF"] + ck, ["nl"])
+        ts(T.nl[:, 0:3], uF, cadd, A.add, ["uF"] + ck, ["nl"])
         bwin = T.booki[:, :]
+        if M == 4:
+            scan(T.osm[:, :], T.sumr[:, :], T.pr[:, :], A.mult, A.add, ["sumr", "pr"], ["osm"])
         cp(T.bkl[:, :], bwin.indirect(T.nl[:, 0:3]), ["bookA", "bookB", "nl"], ["bkl"])
+        if M == 4:
+            ts(T.owno[:, :], T.osm[:, 19:120:20], -1.0, A.add, ["osm"], ["owno"])
+            ts(T.zz[:, :], T.osm[:, 19:120:20], 0.0, A.is_equal, ["osm"], ["zz"], 16387.0, A.mult)
         act(T.zc[:, 384:768], Zall.indirect(T.bkl[:, 24:48]), Zk + ["bkl"], ["zcS"])
         cp(T.zc[:, 0:384], Zall.indirect(T.bkl[:, 0:24]), Zk + ["bkl"], ["zcV"])
         if t == 0:
+            cp(T.blist[:, 0:1024 - 2 * PH:2], T.booki[:, PH:512], ["bookA"], ["blist"])
+            cp(T.blist[:, 1:1024 - 2 * PH:2], T.booki[:, 512 + PH:1024], ["bookA"], ["blist"])
             sinit(2048, 4096, "S1")
         for p in range(16):
             mm(T.ps4[0:48, p:256:16], T.zc[:, p:768:16], T.scw[:, :], ["zcS", "zcV", "scw"], ["B4"])
-        ts(T.ko[:, :], T.selo[:, 63:96:16], C[:, 8:9], A.subtract, ["selo", "c8"], ["ko"], -1.0, A.mult)
         if M == 4:
-            for jb in range(3):
-                ts(T.eqo[:, 20 * jb:20 * jb + 20], T.iof[:, 0:20], T.ko[:, jb:jb + 1], A.is_equal, ["iof", "ko"], ["eqo"])
-        ts(T.nl6[:, 0:6:2], T.uF[:, :], cadd, A.add, ["uF"] + ck, ["nl6"])
-        ts(T.nl6[:, 1:6:2], T.uF[:, :], cadd, A.add, ["uF"] + ck, ["nl6"])
-        if M == 4:
-            tt(T.pr[:, 0:60], st[:, 60:120], T.eqo[:, :], A.mult, [stk, "eqo"], ["pr"])
-            tt(T.pr[:, 60:120], st[:, 120:180], T.eqo[:, :], A.mult, [stk, "eqo"], ["pr"])
-        cp(T.bk2[:, :], bwin.indirect(T.nl6[:, :]), ["bookA", "bookB", "nl6"], ["bk2"])
-        if M == 4:
-            scan(T.osm[:, :], T.sumr[:, :], T.pr[:, :], A.mult, A.add, ["sumr", "pr"], ["osm"])
-            ts(T.owno[:, :], T.osm[:, 19:120:20], -1.0, A.add, ["osm"], ["owno"])
-            ts(T.zz[:, :], T.osm[:, 19:120:20], 0.0, A.is_equal, ["osm"], ["zz"], 4097.0, A.mult)
             tt(T.f6[:, :], T.owno[:, :], T.zz[:, :], A.add, ["owno", "zz"], ["f6"])
             for jb in range(3):
-                for o in range(2):
-                    c = 32 * jb + 16 * o
-                    E("s", lambda e, c=c, j=3 * o + jb: e.activation(out=T.dd[:, c:c + 16], in_=T.dm[:, 0:16], func=AF.Copy, scale=T.f6[:, j:j + 1]), ["dm", "f6"], ["dd"])
-            mm(T.ps7[:, 0:96], T.bof[:, :], T.dd[:, :], ["bof", "dd"], ["B7"])
+                E("s", lambda e, jb=jb: e.activation(out=T.dd[:, 32 * jb:32 * jb + 16], in_=T.dm[:, 0:16], func=AF.Copy, scale=T.f6[:, jb:jb + 1]), ["dm", "f6"], ["ddS"])
+            for jb in range(3):
+                ts(T.dd[:, 32 * jb + 16:32 * jb + 32], T.dm[:, 0:16], T.f6[:, 3 + jb:4 + jb], A.mult, ["dm", "f6"], ["ddV"])
         scan(T.sk[0:48, :], T.srst[0:48, :], T.ps4[0:48, 0:256], A.add, A.max, ["srst", "B4"], ["sk"])
         cp(T.ki[0:48, :], T.sk[0:48, 15:256:16], ["sk"], ["ki"])
+        ts(T.nl6[:, 0:6:2], uF, cadd, A.add, ["uF"] + ck, ["nl6"])
+        if M == 4:
+            ts(T.owno2[:, :], T.owno[:, :], C[:, 10:11], A.add, ["owno", "c10"], ["owno2"])
         ts(T.kia[0:48, :], T.ki[0:48, :], 15, A.bitwise_and, ["ki"], ["kia"])
+        ts(T.nl6[:, 1:6:2], uF, cadd, A.add, ["uF"] + ck, ["nl6"])
         cp(T.kb[0:48, :], T.kia[0:48, :], ["kia"], ["kb"])
+        cp(T.bk2[:, :], bwin.indirect(T.nl6[:, :]), ["bookA", "bookB", "nl6"], ["bk2"])
         mm(T.ps6[0:8, 0:96], T.kb[0:48, 0:8], T.pmx[0:48, 0:96], ["kb", "pmx"], ["B6"], True, False)
         mm(T.ps6[0:8, 0:96], T.kb[0:48, 8:16], T.pmx[0:48, 96:192], ["kb", "pmx"], ["B6"], False, True)
-        if M == 4:
-            for jb in range(3):
-                cp(T.fn[:, 64 * jb + 32:64 * jb + 64], T.ps7[:, 32 * jb:32 * jb + 32], ["B7"], ["fn"])
         cp(T.xp[0:8, :], T.ps6[0:8, 0:96], ["B6"], ["xp"])
         mm(T.ps6[:, 96:192], T.e8[0:8, :], T.xp[0:8, :], ["e8", "xp"], ["B6"])
+        if M == 4:
+            mm(T.ps7[:, 0:96], T.bof[:, :], T.dd[:, :], ["bof", "ddS", "ddV"], ["B7"])
         ts(T.em[:, :], T.ps6[:, 96:192], C[:, 4:5], A.is_equal, ["B6", "c4"], ["em"])
         tt(T.mb[:, :], T.em[:, :], T.bk2[:, :], A.mult, ["em", "bk2"], ["mb"])
         mm(T.ps6[:, 192:288], T.bof[:, :], T.mb[:, :], ["bof", "mb"], ["B6"])
         if M == 4:
-            ts(T.prs[:, :], T.osm[:, 19:120:20], 0.0, A.is_gt, ["osm"], ["prs"])
-            tt(T.zz[:, :], T.owno[:, :], T.padf[:, 6:12], A.subtract, ["owno", "padf"], ["zz"])
-            tt(T.dn[:, 6:12], T.zz[:, :], T.prs[:, :], A.mult, ["zz", "prs"], ["dnO"])
-        scan(T.nsel[:, :], T.selc[:, :], T.ps6[:, 192:288], A.add, A.max, ["selc", "B6"], ["nsel"])
+            for jb in range(3):
+                ts(T.fn[:, 64 * jb + 32:64 * jb + 64], T.ps7[:, 32 * jb:32 * jb + 32], C[:, 10:11], A.add, ["B7", "c10"], ["fn"])
+            for o in range(2):
+                tt(T.dn[:, 2 + o:12:4], T.f6[:, 3 * o:3 * o + 3], T.pad8[:, 14 + o:24:4], A.subtract, ["f6", "pad8"], ["dnO"])
+        scan(T.nsel[:, :], T.selc2[:, :], T.ps6[:, 192:288], A.add, A.max, ["selc2", "B6"], ["nsel"])
         R = 16 * M
         if M == 2:
-            cp(T.fn[:, 0:96], T.ps6[:, 192:288], ["B6"], ["fn"])
+            ts(T.fn[:, 0:96], T.ps6[:, 192:288], C[:, 10:11], A.add, ["B6", "c10"], ["fn"])
         else:
             for jb in range(3):
-                cp(T.fn[:, 64 * jb:64 * jb + 32], T.ps6[:, 192 + 32 * jb:224 + 32 * jb], ["B6"], ["fn"])
-        ts(T.ownn[:, :], T.nsel[:, 15:96:16], C[:, 3:4], A.subtract, ["nsel", "c3"], ["ownn"])
+                ts(T.fn[:, 64 * jb:64 * jb + 32], T.ps6[:, 192 + 32 * jb:224 + 32 * jb], C[:, 10:11], A.add, ["B6", "c10"], ["fn"])
+        def early(now):
+            if not now:
+                return
+            ts(uN, uF, cadd, A.add, ["uF"] + ck, ["uN"])
+            ts(T.kz[:, :], T.ko[:, :], 20.0, A.is_equal, ["ko"], ["kz"], float(t + 1 - 20), A.mult)
+            ts(T.val6[:, :], T.ownn[:, :], 1.0, A.add, ["ownn"], ["val6"])
+            ts(uM, uN, 1023, A.bitwise_and, ["uN"], ["uM"])
+            tt(T.kst[:, :], T.kz[:, :], T.ko[:, :], A.add, ["kz", "ko"], ["kst"])
+            cp(T.nK[:, :], uM, ["uM"], ["nK"])
+            for jb in range(3):
+                ts(T.neq[:, 20 * jb:20 * jb + 20], T.iof[:, 0:20], T.kst[:, jb:jb + 1], A.not_equal, ["iof", "kst"], ["neq"])
+            for jb in range(3):
+                ts(T.xs[:, 20 * jb:20 * jb + 20], T.iof[:, 0:20], T.kst[:, jb:jb + 1], A.is_equal, ["iof", "kst", "nK"], ["xs"], T.nK[:, jb:jb + 1], A.mult)
+            if last:
+                ts(T.lzz[:, 0:120], st[:, 60:180], -1.0, A.add, [stk], ["lz"])
+            for a in range(3):
+                old = st[:, 60 * a:60 * a + 60] if a == 0 or not last else T.lzz[:, 60 * a - 60:60 * a]
+                tt(T.ts3[:, 60 * a:60 * a + 60], old, T.neq[:, :], A.mult, [stk, "neq", "lz"] + (["st0n"] if t == 0 else []), ["ts3"])
+            if last:
+                fin_part(0)
+
+        def fin_part(a):
+            for jb in range(3):
+                c = 60 * a + 20 * jb
+                tt(T.sf[:, 60 * a + jb:60 * a + 60:3], T.ts3[:, c:c + 20], T.xs[:, c:c + 20], A.add, ["ts3", "xs"], ["sf"])
+
         tiles = []
         for jb in range(3):
             for m in range(M):
-                col = T.ownn[:, 2 * jb + m:2 * jb + m + 1] if m < 2 else T.owno[:, 3 * (m - 2) + jb:3 * (m - 2) + jb + 1]
+                e = 15 + 16 * (2 * jb + m)
+                col = T.nsel[:, e:e + 1] if m < 2 else T.owno2[:, 3 * (m - 2) + jb:3 * (m - 2) + jb + 1]
                 b = 192 * len(tiles)
                 key = "e_%d" % len(tiles)
-                ts(T.eqb[:, b:b + R * (3 - jb)], T.fn[:, R * jb:3 * R], col, A.is_equal, ["fn", "ownn", "owno"] if m >= 2 else ["fn", "ownn"], [key])
+                ts(T.eqb[:, b:b + R * (3 - jb)], T.fn[:, R * jb:3 * R], col, A.is_equal, ["fn", "nsel", "owno2"] if m >= 2 else ["fn", "nsel"], [key])
                 tiles.append((jb, b, key))
+            if jb == 0:
+                ts(T.ownn[:, :], T.nsel[:, 15:96:16], C[:, 10:11], A.subtract, ["nsel", "c10"], ["ownn"])
         for jb in range(3):
             todo = [(T.bob, "bob", b + R * (jb - j2), key) for (j2, b, key) in tiles if j2 < jb] + [(T.thr, "thr", b, key) for (j2, b, key) in tiles if j2 == jb]
             for i in range(len(todo)):
                 wm, wk, b, key = todo[i]
                 mm(T.ps7[:, 128 + R * jb:128 + R * jb + R], wm[:, :], T.eqb[:, b:b + R], [wk, key], ["B7"], i == 0, i == len(todo) - 1)
         LW = 3 * M
-        cp(T.pl[:, 0:6:2], T.ownn[:, 1:6:2], ["ownn"], ["pl"])
-        cp(T.pl[:, 1:6:2], T.ownn[:, 0:6:2], ["ownn"], ["pl"])
+        cp(T.pl[:, 0:LW:M], T.ownn[:, 1:6:2], ["ownn"], ["pl"])
+        cp(T.pl[:, 1:LW:M], T.ownn[:, 0:6:2], ["ownn"], ["pl"])
         if M == 4:
-            cp(T.pl[:, 6:9], T.owno[:, 3:6], ["owno"], ["pl"])
-            cp(T.pl[:, 9:12], T.owno[:, 0:3], ["owno"], ["pl"])
+            cp(T.pl[:, 2:12:4], T.owno[:, 3:6], ["owno"], ["pl"])
+            cp(T.pl[:, 3:12:4], T.owno[:, 0:3], ["owno"], ["pl"])
         if not last:
             act(T.zp[:, 0:16 * LW], Zall.indirect(T.pl[:, 0:LW]), Zk + ["pl"], ["zp"])
         act(T.sp[:, 0:16 * LW], T.S[:, :].indirect(T.pl[:, 0:LW]), Sk + ["pl"], ["sp"])
-        tt(T.dn[:, 0:6], T.ownn[:, :], T.padf[:, 0:6], A.subtract, ["ownn", "padf"], ["dnN"])
+        for s_ in range(2):
+            tt(T.dn[:, s_:LW:M], T.ownn[:, s_:6:2], T.pad8[:, 12 + s_:12 + LW:M], A.subtract, ["ownn", "pad8"], ["dnN"])
+        early(last)
         tt(T.cm[:, 0:3 * R], T.ps7[:, 128:128 + 3 * R], T.dm[:, 0:3 * R], A.mult, ["B7", "dm"], ["cm"])
         for jb in range(3):
             red(T.m3[:, jb:jb + 1], T.cm[:, R * jb:R * jb + R], A.max, ["cm"], ["m3"])
-        for q in range(2):
-            ts(T.acc[:, q:6:2], T.m3[:, :], 1.5, A.is_lt, ["m3"], ["acc"])
-        if M == 4:
-            for o in range(2):
-                ts(T.acc[:, 6 + 3 * o:9 + 3 * o], T.m3[:, :], 1.5, A.is_lt, ["m3"], ["acc"])
         dk = ["dnN", "dnO"] if M == 4 else ["dnN"]
-        tt(T.of1[:, 0:LW], T.dn[:, 0:LW], T.acc[:, 0:LW], A.mult, dk + ["acc"], ["of1"])
-        tt(T.of2[:, 0:LW], T.of1[:, 0:LW], T.padf[:, 0:LW], A.add, ["of1", "padf"], ["of2"])
+        for jb in range(3):
+            ts(T.of1[:, M * jb:M * jb + M], T.dn[:, M * jb:M * jb + M], T.m3[:, jb:jb + 1], A.add, dk + ["m3"], ["of1"], 0.0, A.min)
+        tt(T.of2[:, 0:LW], T.of1[:, 0:LW], T.pad8[:, 0:LW], A.add, ["of1", "pad8"], ["of2"])
         cp(T.offs[:, 0:LW], T.of2[:, 0:LW], ["of2"], ["offs"])
         if not last:
             cp(Zall.indirect(T.offs[:, 0:LW]), T.zp[:, 0:16 * LW], ["offs", "zp"], Zk)
-        ts(T.uN[:, :], T.uF[:, :], cadd, A.add, ["uF"] + ck, ["uN"])
-        ts(T.kz[:, :], T.ko[:, :], 20.0, A.is_equal, ["ko"], ["kz"], float(t + 1 - 20), A.mult)
-        ts(T.val6[:, :], T.ownn[:, :], 1.0, A.add, ["ownn"], ["val6"])
-        ts(T.uM[:, :], T.uN[:, :], 1023, A.bitwise_and, ["uN"], ["uM"])
-        tt(T.kst[:, :], T.kz[:, :], T.ko[:, :], A.add, ["kz", "ko"], ["kst"])
+        if not last:
+            ts(T.hitb[:, :], T.ko[:, :], 19.5, A.is_lt, ["ko"], ["hitb"])
+            mm(T.ps7[:, 384:387], T.onb[:, :], T.hitb[:, :], ["onb", "hitb"], ["B7"])
+        early(not last)
+        for q in range(2):
+            ts(T.acc[:, q:6:2], T.m3[:, :], 12288.0, A.is_lt, ["m3"], ["acc"])
         tt(T.ab6[:, :], T.val6[:, :], T.acc[:, 0:6], A.mult, ["val6", "acc"], ["ab6"])
-        cp(T.nK[:, :], T.uM[:, :], ["uM"], ["nK"])
+        if last:
+            ts(T.ab6[:, :], T.ab6[:, :], -1.0, A.add, ["ab6"], ["ab6"])
         for jb in range(3):
-            kc = T.kst[:, jb:jb + 1]
-            ts(T.neq[:, 20 * jb:20 * jb + 20], T.iof[:, 0:20], kc, A.not_equal, ["iof", "kst"], ["neq"])
-        for jb in range(3):
-            kc = T.kst[:, jb:jb + 1]
-            for a in range(3):
-                v = T.nK[:, jb:jb + 1] if a == 0 else T.ab6[:, 2 * jb + a - 1:2 * jb + a]
+            for a in range(1, 3):
                 c = 60 * a + 20 * jb
-                ts(T.xs[:, c:c + 20], T.iof[:, 0:20], kc, A.is_equal, ["iof", "kst", "nK", "ab6"], ["xs"], v, A.mult)
-        for a in range(3):
-            tt(T.ts3[:, 60 * a:60 * a + 60], st[:, 60 * a:60 * a + 60], T.neq[:, :], A.mult, [stk, "neq"] + (["st0n"] if t == 0 else []), ["ts3"])
+                ts(T.xs[:, c:c + 20], T.iof[:, 0:20], T.kst[:, jb:jb + 1], A.is_equal, ["iof", "kst", "ab6"], ["xs"], T.ab6[:, 2 * jb + a - 1:2 * jb + a], A.mult)
         if not last:
             sok = "so%d" % t
             tt(T[sok][:, :], T.ts3[:, :], T.xs[:, :], A.add, ["ts3", "xs"], [sok])
             dst, src_ap = nxt, T[sok][:, :]
         else:
-            tt(T.ts3[:, :], T.ts3[:, :], T.xs[:, :], A.add, ["ts3", "xs"], ["ts3"])
-            for a in range(3):
-                for jb in range(3):
-                    o_, i_ = T.sf[:, 60 * a + jb:60 * a + 60:3], T.ts3[:, 60 * a + 20 * jb:60 * a + 20 * jb + 20]
-                    ts(o_, i_, 0.0 if a == 0 else -1.0, A.add, ["ts3"], ["sf"])
+            fin_part(1)
+            fin_part(2)
             sok = "sf"
             dst, src_ap = prv, T.sf[:, :]
         deps("g", [sok], [])
@@ -428,15 +507,15 @@ def rank_program(g, core, T, topo):
         if last:
             dma("y", T.ys[:, :], T.S[0:128:16, 0:4096], "dout", Sk, [])
             break
-        ts(T.hitb[:, :], T.ko[:, :], 19.5, A.is_lt, ["ko"], ["hitb"])
-        mm(T.ps7[:, 384:387], T.onb[:, :], T.hitb[:, :], ["onb", "hitb"], ["B7"])
         red(T.cc[:, :], T.ps7[:, 384:387], A.add, ["B7"], ["cc"])
-        yphase(lambda t=t: lists(t + 1))
+        if t == 0:
+            cp(T.la[:, :], T.lai[:, :], ["lai"], ["la"])
+        yphase(lambda i, t=t: lists(t + 1, i))
 
     fin = T["st%d" % VI]
     k = "st%d" % VI
     dma("y", T.yk[:, :], fin[:, 0:60], "dout", [k], [])
-    dma("y", T.ya[:, :], fin[:, 60:120], "dout", [k], [])
+    dma("s", T.ya[:, :], fin[:, 60:120], "dout", [k], [])
     dma("y", T.yb[:, :], fin[:, 120:180], "dout", [k], [])
     need("y", "dout", 64)
     need("g", "lsem", cnt["sent"])

from concourse.bass import DstId, RemoteDMATransfer
from concourse.mybir import dt, AluOpType, AxisListType, ActivationFunctionType

VI = 6
PADC = 4288
PH = 344
P_CH = [96, 120, 128]
S_CH = [128, 104, 68, 28, 8]
S0_CH = [128, 128, 128, 128, 128, 80, 48, 16]
V0_CH = [128, 112]
YW = 1 + 16 * 1024
B1, B2 = float(2 ** 23), float(2 ** 21)

_sb = {
    "truv": (4096, "bfloat16"), "Z": (PADC, "bfloat16"), "S": (PADC, "float32"), "iot": (4096, "float32"),
    "booki": (1408, "int32"), "blist": (1024 - 2 * PH, "uint16"), "sgi": (256, "int32"), "sgl": (256, "uint16"),
    "kmi": (64, "int32"),
    "G": (16384, "bfloat16"), "blist0": (1024, "uint16"), "H": (16 * PH, "bfloat16"), "ysc": (YW, "bfloat16"), "rst": (2048, "bfloat16"), "rst8": (2048, "bfloat16"),
    "lai": (PH, "int32"), "lbi": (PH, "int32"), "la": (PH, "uint16"), "lb": (PH, "uint16"),
    "lzz": (240, "float32"), "pad8": (24, "float32"),
    "pi": (1, "int32"), "pj": (1, "int32"), "pg": (1, "int32"), "colf": (16, "float32"),
    "iof": (128, "float32"), "iog": (128, "float32"), "ioj": (192, "float32"),
    "idf": (128, "float32"), "idb": (128, "bfloat16"), "bof": (128, "float32"), "bob": (128, "bfloat16"),
    "thr": (128, "bfloat16"), "thf": (128, "float32"), "onb": (128, "bfloat16"), "dm": (192, "float32"),
    "selc": (96, "float32"), "selt": (96, "float32"), "selc2": (96, "float32"), "sel8": (8, "float32"), "cntw": (8, "bfloat16"), "usel": (8, "bfloat16"),
    "scw": (16, "bfloat16"), "pmx": (192, "bfloat16"), "e0": (128, "float32"), "e1": (128, "float32"), "e8": (128, "bfloat16"),
    "srst": (256, "float32"), "kd1": (160, "float32"), "padf": (12, "float32"), "sumr": (120, "float32"),
    "kl": (58, "uint16"), "kl2": (6, "uint16"), "y00": (96, "bfloat16"), "y": (912, "bfloat16"), "lt": (912, "bfloat16"),
    "xx": (160, "float32"), "d1u": (160, "float32"), "su": (320, "float32"), "xt": (48, "float32"), "selo": (96, "float32"),
    "uint": (28, "int32"), "nK": (3, "float32"), "nl": (4, "uint16"), "nl6": (6, "uint16"), "bkl": (48, "uint16"), "bk2": (96, "float32"),
    "zc": (768, "bfloat16"), "ko": (3, "float32"), "kz": (3, "float32"), "kst": (3, "float32"), "hitb": (3, "bfloat16"),
    "eqo": (60, "float32"), "pr": (120, "float32"), "osm": (120, "float32"), "owno": (6, "float32"), "owno2": (6, "float32"), "ownn": (6, "float32"),
    "zz": (6, "float32"), "f6": (6, "float32"), "dn": (12, "float32"), "dd": (96, "float32"),
    "sk": (256, "float32"), "ki": (16, "int32"), "kia": (16, "int32"), "kb": (16, "bfloat16"), "xp": (96, "bfloat16"),
    "em": (96, "float32"), "mb": (96, "float32"), "nsel": (96, "float32"), "fn": (192, "uint16"),
    "eqb": (2304, "bfloat16"), "cm": (192, "float32"), "m3": (3, "float32"), "acc": (12, "float32"),
    "of1": (12, "float32"), "of2": (12, "float32"), "offs": (12, "uint16"), "pl": (12, "uint16"),
    "zp": (192, "bfloat16"), "sp": (192, "float32"), "neq": (60, "float32"), "ab6": (6, "float32"), "val6": (6, "float32"),
    "xs": (180, "float32"), "ts3": (180, "float32"), "cc": (1, "float32"), "sf": (180, "float32"),
}
SCRATCH = {}
for _k in _sb:
    SCRATCH[_k] = ("sbuf", [128, _sb[_k][0]], _sb[_k][1])
for _t in range(VI + 1):
    SCRATCH["st%d" % _t] = ("sbuf", [128, 180], "float32")
for _t in range(VI - 1):
    SCRATCH["so%d" % _t] = ("sbuf", [128, 180], "float32")
for _t in range(8):
    SCRATCH["ps%d" % _t] = ("psum", [128, 512], "float32")
SEMAPHORES = ["sv", "ss", "sp_", "sg_", "lsg", "ltr", "lbk", "lbw", "lkm", "lwt", "lhf", "lhg", "dout", "lsem"] + ["arr%d" % _t for _t in range(1, VI + 1)]


def rank_program(g, core, T, topo):
    rank = T.rank_of(core)
    if rank is None:
        return
    A, AX, AF = AluOpType, AxisListType, ActivationFunctionType
    cores = T.cores
    nxt, prv = cores[(rank + 1) % 4], cores[(rank + 3) % 4]

    eng = {"v": g.vector, "s": g.scalar, "p": g.tensor, "g": g, "y": g.sync}
    semn = {"v": "sv", "s": "ss", "p": "sp_", "g": "sg_"}
    cnt = {"v": 0, "s": 0, "p": 0, "g": 0}
    waited = {}
    wr, rd = {}, {}

    def need(q, sem, n):
        if waited.get((q, sem), 0) < n:
            waited[(q, sem)] = n
            eng[q].wait_ge(T.sem[sem], n)

    def deps(q, r, w):
        lst = {}
        for k in r:
            if k in wr:
                sem, n, q2 = wr[k]
                if not (q == "p" and q2 == "p"):
                    lst[sem] = max(lst.get(sem, 0), n)
        for k in w:
            if k in wr and wr[k][2] != q:
                lst[wr[k][0]] = max(lst.get(wr[k][0], 0), wr[k][1])
            for (sem, n, q2) in rd.get(k, {}).values():
                if q2 != q or q == "v":
                    lst[sem] = max(lst.get(sem, 0), n)
        for sem in lst:
            need(q, sem, lst[sem])

    def note(q, r, w, tag):
        for k in r:
            rd.setdefault(k, {})[q] = tag
        for k in w:
            wr[k] = tag
            rd[k] = {}

    def E(q, f, r, w):
        deps(q, r, w)
        i = f(eng[q])
        cnt[q] += 1
        i.then_inc(T.sem[semn[q]], 1)
        note(q, r, w, (semn[q], cnt[q], q))

    def dma(q, out, in_, sem, r, w):
        deps(q, r, w)
        eng[q].dma_start(out=out, in_=in_).then_inc(T.sem[sem], 16)
        note(q, r, w, (sem, 16, "dma"))

    def ts(out, in0, s1, op0, r, w, s2=None, op1=None):
        if op1 is None:
            E("v", lambda e: e.tensor_scalar(out=out, in0=in0, scalar1=s1, scalar2=None, op0=op0), r, w)
        else:
            E("v", lambda e: e.tensor_scalar(out=out, in0=in0, scalar1=s1, scalar2=s2, op0=op0, op1=op1), r, w)

    def tt(out, a, b, op, r, w):
        E("v", lambda e: e.tensor_tensor(out=out, in0=a, in1=b, op=op), r, w)

    def cp(out, a, r, w):
        E("v", lambda e: e.tensor_copy(out=out, in_=a), r, w)

    def scan(out, d0, d1, op0, op1, r, w):
        E("v", lambda e: e.tensor_tensor_scan(out=out, data0=d0, data1=d1, initial=0.0, op0=op0, op1=op1), r, w)

    def red(out, a, op, r, w):
        E("v", lambda e: e.tensor_reduce(out=out, in_=a, axis=AX.X, op=op), r, w)

    def ms(ap, c, w, r=()):
        E("v", lambda e: e.memset(ap, c), r, w)

    def act(out, a, r, w, **kw):
        E("s", lambda e: e.activation(out=out, in_=a, func=AF.Copy, **kw), r, w)

    def mm(out, lhsT, rhs, r, w, start=True, stop=True):
        E("p", lambda e: e.matmul(out, lhsT, rhs, start, stop), r, w)

    def iota(out, pattern, base, cm, w):
        E("g", lambda e: e.iota(out, pattern, base, cm, allow_small_or_imprecise_dtypes=True), [], w)

    dma("y", T.sgi[:, :], T.sg0[:, :], "lsg", [], ["sgi"])
    dma("y", T.truv[:, :], T.tru[:, :], "ltr", [], ["truv"])
    dma("s", T.booki[:, 0:1024], T.book[:, :], "lbk", [], ["bookA"])
    dma("y", T.kmi[:, 60:61], T.wt[:, :], "lwt", [], ["wti"])
    dma("y", T.kmi[:, 0:60], T.km0[:, :], "lkm", [], ["kmi"])
    dma("y", T.booki[:, 1024:1408], T.book[:, 0:384], "lbw", [], ["bookB"])

    def halves(q, buf, o, key, sem):
        for p in range(8):
            for h in range(2):
                eng[q].dma_start(out=buf[p + 8 * h:128:16, :], in_=T.book[p + o:128:16, 512 * h:512 * h + PH]).then_inc(T.sem[sem], 16)
        note(q, [], [key], (sem, 256, "dma"))

    halves("y", T.lbi, 8, "lbi", "lhf")

    cp(T.sgl[:, :], T.sgi[:, :], ["sgi"], ["sgl"])
    ms(T.Z[:, 4096:PADC], 0.0, ["Zpad"])
    ms(T.rst[:, :], 0.0, ["rst"])
    ms(T.rst8[:, :], 0.0, ["rst8"])
    ms(T.rst[:, 0:2048:16], 512.0, ["rst"], ["rst"])
    ms(T.rst8[:, 0:2048:8], 512.0, ["rst8"], ["rst8"])
    ms(T.ysc[:, 0:1], 0.0, ["Y0"])
    iota(T.pi[:, :], [[0, 1]], 0, 1, ["pi"])
    iota(T.iof[:, :], [[1, 128]], 0, 0, ["iof"])
    iota(T.iog[:, :], [[1, 8], [0, 16]], 0, 0, ["iog"])
    iota(T.ioj[:, :], [[0, 12], [1, 16]], 0, 0, ["ioj"])
    iota(T.kd1[:, :], [[0, 8], [1, 20]], 256, 0, ["kd1"])
    iota(T.padf[:, :], [[16, 12]], 4096, 0, ["padf"])
    iota(T.iot[:, :], [[1, 4096]], 0, 0, ["iot"])
    halves("g", T.lai, 0, "lai", "lhg")
    act(T.Z[:, 0:2048], T.truv[:, :].indirect(T.sgl[:, 0:128]), ["truv", "sgl"], ["ZA"])
    Zk = ["ZA", "ZB", "Zpad"]
    Zall = T.Z[:, :]

    def yphase(before_tail):
        c, pits, sits = 0, [], []
        for i in range(len(P_CH)):
            pits.append((c, P_CH[i], "G%d" % i, "H%d" % i))
            c += P_CH[i]
        for i in range(len(S_CH)):
            sits.append((c, S_CH[i], "J%d" % i))
            c += S_CH[i]
        for (c, n, k, k2) in pits:
            act(T.G[:, 16 * c:16 * (c + n)], Zall.indirect(T.lb[:, c:c + n]), Zk + ["lb"], [k])
        for (c, n, k) in sits:
            act(T.G[:, 16 * c:16 * (c + n)], Zall.indirect(T.blist[:, c - PH:c - PH + n]), Zk + ["blist"], [k])
        for (c, n, k, k2) in pits:
            tt(T.H[:, 16 * c:16 * (c + n)], Zall.indirect(T.la[:, c:c + n]), T.G[:, 16 * c:16 * (c + n)], A.min, Zk + ["la", k], [k2])
        for (c, n, k, k2) in pits:
            scan(T.ysc[:, 1 + 16 * c:1 + 16 * (c + n)], T.rst8[:, 0:16 * n], T.H[:, 16 * c:16 * (c + n)], A.max, A.min, ["rst8", k2], ["Y"])
        for i in range(len(sits)):
            (c, n, k) = sits[i]
            before_tail(i)
            scan(T.ysc[:, 1 + 16 * c:1 + 16 * (c + n)], T.rst[:, 0:16 * n], T.G[:, 16 * c:16 * (c + n)], A.max, A.min, ["rst", k], ["Y"])

    def lists(t, i):
        st = T["st%d" % t]
        sk_ = "st%d" % t
        lz, lz2, lw = T.lzz[:, 0:60], T.lzz[:, 60:120], T.lzz[:, 120:180]
        if i == 0:
            ts(lz, st[:, 0:60], 511.5, A.is_ge, [sk_], ["lz"], -511.5, A.mult)
        if i == 1:
            tt(lz2, st[:, 0:60], lz, A.add, [sk_, "lz"], ["lz2"])
        if i == 2:
            ts(lw, lz2, -(PH - 0.5), A.add, ["lz2"], ["lw"], 0.0, A.max)
        if i == 3:
            tt(T.lzz[:, 180:240], lz2, lw, A.add, ["lz2", "lw"], ["lz3"])
        if i < 4:
            return
        ts(T.kl2[:, 0:3], T.lzz[:, 180:240:20], 16.0, A.mult, ["lz3"], ["kl2"], 8.0, A.add)
        ts(T.kl2[:, 3:6], T.lzz[:, 180:240:20], 16.0, A.mult, ["lz3"], ["kl2"], 8.0, A.add)
        for jb in range(3):
            ts(T.kl[:, jb:57:3], T.lzz[:, 181 + 20 * jb:200 + 20 * jb], 16.0, A.mult, ["lz3"], ["kl"], 8.0, A.add)

    def consts():
        C = T.colf
        ts(T.pj[:, :], T.pi[:, :], 15, A.bitwise_and, ["pi"], ["pj"])
        ts(T.pg[:, :], T.pi[:, :], 4, A.arith_shift_right, ["pi"], ["pg"])
        cp(C[:, 0:1], T.pi[:, :], ["pi"], ["c0"])
        cp(C[:, 1:2], T.pj[:, :], ["pj"], ["c1"])
        cp(C[:, 2:3], T.pg[:, :], ["pg"], ["c2"])
        cp(C[:, 9:10], T.kmi[:, 60:61], ["wti"], ["c9"])
        ts(C[:, 3:4], C[:, 1:2], 14.5, A.is_lt, ["c1"], ["c3"], B2, A.mult)
        ts(C[:, 4:5], C[:, 1:2], -1.0, A.mult, ["c1"], ["c4"], 15.0, A.add)
        ts(C[:, 5:6], C[:, 2:3], 16.0, A.mult, ["c2"], ["c5"], C[:, 0:1], A.add)
        ts(C[:, 6:7], C[:, 5:6], 16.0, A.add, ["c5"], ["c6"])
        ts(C[:, 7:8], C[:, 0:1], -8.0, A.add, ["c0"], ["c7"])
        ts(C[:, 8:9], C[:, 3:4], 276.0, A.add, ["c3"], ["c8"])
        ts(T.sel8[:, :], T.iof[:, 0:8], C[:, 2:3], A.is_equal, ["iof", "c2"], ["sel8"])
        ts(T.cntw[:, :], T.sel8[:, :], 32.0, A.mult, ["sel8"], ["cntw"])
        ts(T.usel[:, :], T.sel8[:, :], C[:, 9:10], A.mult, ["sel8", "c9"], ["usel"])
        ts(T.scw[:, 0:8], T.sel8[:, :], 16.0, A.mult, ["sel8"], ["scw"])
        ts(T.scw[:, 8:16], T.sel8[:, :], -16.0, A.mult, ["sel8"], ["scw"])
        ts(T.idf[:, :], T.iof[:, :], C[:, 0:1], A.is_equal, ["iof", "c0"], ["idf"])
        ts(T.idb[:, :], T.iof[:, :], C[:, 0:1], A.is_equal, ["iof", "c0"], ["idb"])
        ts(T.bof[:, :], T.iog[:, :], C[:, 2:3], A.is_equal, ["iog", "c2"], ["bof"])
        ts(T.bob[:, :], T.iog[:, :], C[:, 2:3], A.is_equal, ["iog", "c2"], ["bob"], 8192.0, A.mult)
        ts(T.thf[:, :], T.ioj[:, 0:128], C[:, 1:2], A.is_ge, ["ioj", "c1"], ["thf"], 8192.0, A.mult)
        tt(T.thr[:, :], T.thf[:, :], T.bof[:, :], A.mult, ["thf", "bof"], ["thr"])
        ms(T.onb[:, :], 1.0, ["onb"])
        ts(T.dm[:, :], T.ioj[:, :], C[:, 1:2], A.is_equal, ["ioj", "c1"], ["dm"])
        ts(T.selt[:, :], T.ioj[:, 0:96], C[:, 1:2], A.is_le, ["ioj", "c1"], ["selt"], -B1, A.mult)
        ts(T.selc[:, :], T.ioj[:, 0:96], C[:, 1:2], A.subtract, ["ioj", "c1"], ["selc"], 1.0, A.is_equal)
        ts(T.selc[:, :], T.selc[:, :], B2, A.mult, ["selc"], ["selc"])
        tt(T.selc[:, :], T.selc[:, :], T.selt[:, :], A.add, ["selc", "selt"], ["selc"])
        ts(C[:, 10:11], C[:, 1:2], 14.5, A.is_lt, ["c1"], ["c10"], 8192.0, A.mult)
        ts(T.selt[:, :], T.ioj[:, 0:96], C[:, 1:2], A.is_le, ["ioj", "c1"], ["selt"], -131072.0, A.mult)
        ts(T.selc2[:, :], T.ioj[:, 0:96], C[:, 1:2], A.subtract, ["ioj", "c1"], ["selc2"], 1.0, A.is_equal)
        ts(T.selc2[:, :], T.selc2[:, :], 8192.0, A.mult, ["selc2"], ["selc2"])
        tt(T.selc2[:, :], T.selc2[:, :], T.selt[:, :], A.add, ["selc2", "selt"], ["selc2"])
        ts(T.pmx[0:48, 0:96], T.iof[0:48, 0:96], C[0:48, 5:6], A.is_equal, ["iof", "c5"], ["pmx"])
        ts(T.pmx[0:48, 96:192], T.iof[0:48, 0:96], C[0:48, 6:7], A.is_equal, ["iof", "c6"], ["pmx"])
        ts(T.e0[0:16, :], T.iog[0:16, :], C[0:16, 0:1], A.is_equal, ["iog", "c0"], ["e0"])
        ts(T.e1[0:16, :], T.iog[0:16, :], C[0:16, 7:8], A.is_equal, ["iog", "c7"], ["e1"])
        ts(T.e8[0:8, :], T.iog[0:8, :], C[0:8, 0:1], A.is_equal, ["iog", "c0"], ["e8"])
        ms(T.srst[:, :], 1.0, ["srst"])
        ms(T.srst[:, 0:256:16], -1048576.0, ["srst"], ["srst"])
        ms(T.sumr[:, :], 1.0, ["sumr"])
        ms(T.sumr[:, 0:120:20], 0.0, ["sumr"], ["sumr"])
        ts(T.pad8[:, 0:12], T.padf[:, :], C[:, 1:2], A.add, ["padf", "c1"], ["pad8"])
        ts(T.pad8[:, 12:24], T.padf[:, :], C[:, 1:2], A.add, ["padf", "c1"], ["pad8"], 8192.0, A.add)
        ms(T.S[:, 4096:PADC], 0.0, ["Spad"])
        ms(T.ps3[:, 0:160], 512.0, ["B3"])
        ms(T.st0[:, 60:180], 0.0, ["st0n"])
        for jb in range(3):
            cp(T.st0[:, 20 * jb:20 * jb + 20], T.kmi[:, jb:60:3], ["kmi"], ["st0"])

    cp(T.blist0[:, :], T.booki[:, 0:1024], ["bookA"], ["blist0"])
    cp(T.Z[:, 2048:4096], T.truv[:, :].indirect(T.sgl[:, 128:256]), ["truv", "sgl"], ["ZB"])
    c, its = 0, []
    for (chs, nm) in ((S0_CH, "J"), (V0_CH, "V")):
        for i in range(len(chs)):
            its.append((c, chs[i], nm + "0%d" % i, nm))
            c += chs[i]
    for (c, n, k, nm) in its:
        (act if nm == "J" else cp)(T.G[:, 16 * c:16 * (c + n)], Zall.indirect(T.blist0[:, c:c + n]), Zk + ["blist0"], [k])
    consts()
    for jb in range(3):
        ts(T.kl[:, jb:57:3], T.st0[:, 20 * jb + 1:20 * jb + 20], 16.0, A.mult, ["st0"], ["kl"], 16.0, A.add)
    for i in range(2):
        ts(T.kl2[:, 3 * i:3 * i + 3], T.st0[:, 0:60:20], 16.0, A.mult, ["st0"], ["kl2"], 16.0, A.add)
    for (c, n, k, nm) in its[len(S0_CH):] + its[:len(S0_CH)]:
        scan(T.ysc[:, 1 + 16 * c:1 + 16 * (c + n)], T.rst[:, 0:16 * n], T.G[:, 16 * c:16 * (c + n)], A.max, A.min, ["rst", k], ["Y"])
    for k in ("J", "V"):
        for i in range(8):
            wr.pop(k + "0%d" % i, None)
    Sk = ["S0", "S1", "Spad"]
    C = T.colf
    ywin = T.ysc[:, :]

    def sinit(a, b, key):
        act(T.S[:, a:b], T.iot[:, :].indirect(T.sgl[:, a // 16:b // 16]), ["iot", "sgl"], [key])

    for t in range(VI):
        st, stk = T["st%d" % t], "st%d" % t
        last = t == VI - 1
        M = 2 if t == 0 else 4
        cp(T.y00[:, :], ywin.indirect(T.kl2[:, 0:6]), ["Y", "kl2"], ["y00"])
        act(T.y[:, 384:480], ywin.indirect(T.kl[:, 24:30]), ["Y", "kl"], ["yS1"])
        cp(T.y[:, 0:384], ywin.indirect(T.kl[:, 0:24]), ["Y", "kl"], ["yV"])
        act(T.y[:, 480:912], ywin.indirect(T.kl[:, 30:57]), ["Y", "kl"], ["yS2"])
        if t == 0:
            sinit(0, 2048, "S0")
        for i in range(5):
            mm(T.ps0[:, 96 * i:96 * i + 96], T.idb[:, :], T.y00[:, :], ["idb", "y00"], ["B0"])
        for i in range(5):
            n = 96 if i < 4 else 48
            mm(T.ps1[:, 96 * i:96 * i + n], T.idb[:, :], T.y00[:, 0:n], ["idb", "y00"], ["B1"])

        def yslot(k):
            return T.y[:, 48 * (k - 1):48 * k], ("yV" if k <= 8 else ("yS1" if k <= 10 else "yS2"))

        def usum(k, p):
            ap, key = yslot(k)
            mm(T.ps2[0:48, p:160:20], ap, T.usel[:, :], [key, "usel"], ["B2"])

        def csum(k):
            mm(T.ps3[0:48, 20 - k:160:20], T.lt[:, 48 * (k - 1):48 * k], T.cntw[:, :], ["lt1" if k <= 10 else "lt2", "cntw"], ["B3"])

        usum(1 + t, 0)
        for k in range(1, 11):
            usum(k, 20 - k)
        tt(T.lt[:, 0:480], T.y[:, 0:480], T.ps0[:, 0:480], A.is_lt, ["yV", "yS1", "B0"], ["lt1"])
        for k in range(1, 11):
            csum(k)
        tt(T.lt[:, 480:912], T.y[:, 480:912], T.ps1[:, 0:432], A.is_lt, ["yS2", "B1"], ["lt2"])
        for k in range(11, 20):
            csum(k)
        for k in range(11, 20):
            usum(k, 20 - k)
        if t == 0:
            cp(T.lb[:, :], T.lbi[:, :], ["lbi"], ["lb"])
        ts(T.xx[0:48, :], T.ps3[0:48, 0:160], 272.0, A.is_lt, ["B3"], ["xx"], B2, A.mult)
        scan(T.su[0:48, 160:320], T.ps3[0:48, 0:160], T.kd1[0:48, :], A.max, A.min, ["B3", "kd1"], ["suk"])
        tt(T.d1u[0:48, :], T.ps2[0:48, 0:160], T.xx[0:48, :], A.subtract, ["B2", "xx"], ["d1u"])
        scan(T.su[0:48, 0:160], T.xx[0:48, :], T.d1u[0:48, :], A.min, A.max, ["xx", "d1u"], ["suu"])
        mm(T.ps5[0:16, 0:48], T.su[0:48, 19:320:20], T.idf[0:48, 0:48], ["suk", "suu", "idf"], ["B5"])
        cp(T.xt[0:16, :], T.ps5[0:16, 0:48], ["B5"], ["xt"])
        mm(T.ps5[:, 64:112], T.e0[0:16, :], T.xt[0:16, :], ["e0", "xt"], ["B5"])
        mm(T.ps5[:, 112:160], T.e1[0:16, :], T.xt[0:16, :], ["e1", "xt"], ["B5"])
        scan(T.selo[:, :], T.selc[:, :], T.ps5[:, 64:160], A.add, A.max, ["selc", "B5"], ["selo"])
        uI, uU, uV, uQ, uF, uN, uM = [T.uint[:, 4 * i:4 * i + 3] for i in range(7)]
        def eqold(jb):
            if M == 4:
                ts(T.eqo[:, 20 * jb:20 * jb + 20], T.iof[:, 0:20], T.ko[:, jb:jb + 1], A.is_equal, ["iof", "ko"], ["eqo"])

        def prold(a):
            if M == 4:
                tt(T.pr[:, 60 * a - 60:60 * a], st[:, 60 * a:60 * a + 60], T.eqo[:, :], A.mult, [stk, "eqo"], ["pr"])

        cp(uI, T.selo[:, 15:48:16], ["selo"], ["uI"])
        ts(T.ko[:, :], T.selo[:, 63:96:16], C[:, 8:9], A.subtract, ["selo", "c8"], ["ko"], -1.0, A.mult)
        ts(uU, uI, 4095, A.bitwise_and, ["uI"], ["uU"])
        eqold(0)
        eqold(1)
        ts(uV, uU, 1184.0, A.add, ["uU"], ["uV"])
        eqold(2)
        tt(uQ, uU, uV, A.mult, ["uU", "uV"], ["uQ"])
        prold(1)
        ts(uF, uQ, 5, A.arith_shift_right, ["uQ"], ["uF"], 1023, A.bitwise_and)
        prold(2)
        cadd = 0.0 if t == 0 else T.cc[:, 0:1]
        ck = [] if t == 0 else ["cc"]
        ts(T.nl[:, 0:3], uF, cadd, A.add, ["uF"] + ck, ["nl"])
        bwin = T.booki[:, :]
        if M == 4:
            scan(T.osm[:, :], T.sumr[:, :], T.pr[:, :], A.mult, A.add, ["sumr", "pr"], ["osm"])
        cp(T.bkl[:, :], bwin.indirect(T.nl[:, 0:3]), ["bookA", "bookB", "nl"], ["bkl"])
        if M == 4:
            ts(T.owno[:, :], T.osm[:, 19:120:20], -1.0, A.add, ["osm"], ["owno"])
            ts(T.zz[:, :], T.osm[:, 19:120:20], 0.0, A.is_equal, ["osm"], ["zz"], 16387.0, A.mult)
        act(T.zc[:, 384:768], Zall.indirect(T.bkl[:, 24:48]), Zk + ["bkl"], ["zcS"])
        cp(T.zc[:, 0:384], Zall.indirect(T.bkl[:, 0:24]), Zk + ["bkl"], ["zcV"])
        if t == 0:
            cp(T.blist[:, 0:1024 - 2 * PH:2], T.booki[:, PH:512], ["bookA"], ["blist"])
            cp(T.blist[:, 1:1024 - 2 * PH:2], T.booki[:, 512 + PH:1024], ["bookA"], ["blist"])
            sinit(2048, 4096, "S1")
        for p in range(16):
            mm(T.ps4[0:48, p:256:16], T.zc[:, p:768:16], T.scw[:, :], ["zcS", "zcV", "scw"], ["B4"])
        if M == 4:
            tt(T.f6[:, :], T.owno[:, :], T.zz[:, :], A.add, ["owno", "zz"], ["f6"])
            for jb in range(3):
                E("s", lambda e, jb=jb: e.activation(out=T.dd[:, 32 * jb:32 * jb + 16], in_=T.dm[:, 0:16], func=AF.Copy, scale=T.f6[:, jb:jb + 1]), ["dm", "f6"], ["ddS"])
            for jb in range(3):
                ts(T.dd[:, 32 * jb + 16:32 * jb + 32], T.dm[:, 0:16], T.f6[:, 3 + jb:4 + jb], A.mult, ["dm", "f6"], ["ddV"])
        scan(T.sk[0:48, :], T.srst[0:48, :], T.ps4[0:48, 0:256], A.add, A.max, ["srst", "B4"], ["sk"])
        cp(T.ki[0:48, :], T.sk[0:48, 15:256:16], ["sk"], ["ki"])
        ts(T.nl6[:, 0:6:2], uF, cadd, A.add, ["uF"] + ck, ["nl6"])
        if M == 4:
            ts(T.owno2[:, :], T.owno[:, :], C[:, 10:11], A.add, ["owno", "c10"], ["owno2"])
        ts(T.kia[0:48, :], T.ki[0:48, :], 15, A.bitwise_and, ["ki"], ["kia"])
        ts(T.nl6[:, 1:6:2], uF, cadd, A.add, ["uF"] + ck, ["nl6"])
        cp(T.kb[0:48, :], T.kia[0:48, :], ["kia"], ["kb"])
        cp(T.bk2[:, :], bwin.indirect(T.nl6[:, :]), ["bookA", "bookB", "nl6"], ["bk2"])
        mm(T.ps6[0:8, 0:96], T.kb[0:48, 0:8], T.pmx[0:48, 0:96], ["kb", "pmx"], ["B6"], True, False)
        mm(T.ps6[0:8, 0:96], T.kb[0:48, 8:16], T.pmx[0:48, 96:192], ["kb", "pmx"], ["B6"], False, True)
        cp(T.xp[0:8, :], T.ps6[0:8, 0:96], ["B6"], ["xp"])
        mm(T.ps6[:, 96:192], T.e8[0:8, :], T.xp[0:8, :], ["e8", "xp"], ["B6"])
        if M == 4:
            mm(T.ps7[:, 0:96], T.bof[:, :], T.dd[:, :], ["bof", "ddS", "ddV"], ["B7"])
        ts(T.em[:, :], T.ps6[:, 96:192], C[:, 4:5], A.is_equal, ["B6", "c4"], ["em"])
        tt(T.mb[:, :], T.em[:, :], T.bk2[:, :], A.mult, ["em", "bk2"], ["mb"])
        mm(T.ps6[:, 192:288], T.bof[:, :], T.mb[:, :], ["bof", "mb"], ["B6"])
        if M == 4:
            for jb in range(3):
                ts(T.fn[:, 64 * jb + 32:64 * jb + 64], T.ps7[:, 32 * jb:32 * jb + 32], C[:, 10:11], A.add, ["B7", "c10"], ["fn"])
            for o in range(2):
                tt(T.dn[:, 2 + o:12:4], T.f6[:, 3 * o:3 * o + 3], T.pad8[:, 14 + o:24:4], A.subtract, ["f6", "pad8"], ["dnO"])
        scan(T.nsel[:, :], T.selc2[:, :], T.ps6[:, 192:288], A.add, A.max, ["selc2", "B6"], ["nsel"])
        R = 16 * M
        if M == 2:
            ts(T.fn[:, 0:96], T.ps6[:, 192:288], C[:, 10:11], A.add, ["B6", "c10"], ["fn"])
        else:
            for jb in range(3):
                ts(T.fn[:, 64 * jb:64 * jb + 32], T.ps6[:, 192 + 32 * jb:224 + 32 * jb], C[:, 10:11], A.add, ["B6", "c10"], ["fn"])
        def early(now):
            if not now:
                return
            ts(uN, uF, cadd, A.add, ["uF"] + ck, ["uN"])
            ts(T.kz[:, :], T.ko[:, :], 20.0, A.is_equal, ["ko"], ["kz"], float(t + 1 - 20), A.mult)
            ts(T.val6[:, :], T.ownn[:, :], 1.0, A.add, ["ownn"], ["val6"])
            ts(uM, uN, 1023, A.bitwise_and, ["uN"], ["uM"])
            tt(T.kst[:, :], T.kz[:, :], T.ko[:, :], A.add, ["kz", "ko"], ["kst"])
            cp(T.nK[:, :], uM, ["uM"], ["nK"])
            for jb in range(3):
                ts(T.neq[:, 20 * jb:20 * jb + 20], T.iof[:, 0:20], T.kst[:, jb:jb + 1], A.not_equal, ["iof", "kst"], ["neq"])
            for jb in range(3):
                ts(T.xs[:, 20 * jb:20 * jb + 20], T.iof[:, 0:20], T.kst[:, jb:jb + 1], A.is_equal, ["iof", "kst", "nK"], ["xs"], T.nK[:, jb:jb + 1], A.mult)
            if last:
                ts(T.lzz[:, 0:120], st[:, 60:180], -1.0, A.add, [stk], ["lz"])
            for a in range(3):
                old = st[:, 60 * a:60 * a + 60] if a == 0 or not last else T.lzz[:, 60 * a - 60:60 * a]
                tt(T.ts3[:, 60 * a:60 * a + 60], old, T.neq[:, :], A.mult, [stk, "neq", "lz"] + (["st0n"] if t == 0 else []), ["ts3"])
            if last:
                fin_part(0)

        def fin_part(a):
            for jb in range(3):
                c = 60 * a + 20 * jb
                tt(T.sf[:, 60 * a + jb:60 * a + 60:3], T.ts3[:, c:c + 20], T.xs[:, c:c + 20], A.add, ["ts3", "xs"], ["sf"])

        tiles = []
        for jb in range(3):
            for m in range(M):
                e = 15 + 16 * (2 * jb + m)
                col = T.nsel[:, e:e + 1] if m < 2 else T.owno2[:, 3 * (m - 2) + jb:3 * (m - 2) + jb + 1]
                b = 192 * len(tiles)
                key = "e_%d" % len(tiles)
                ts(T.eqb[:, b:b + R * (3 - jb)], T.fn[:, R * jb:3 * R], col, A.is_equal, ["fn", "nsel", "owno2"] if m >= 2 else ["fn", "nsel"], [key])
                tiles.append((jb, b, key))
            if jb == 0:
                ts(T.ownn[:, :], T.nsel[:, 15:96:16], C[:, 10:11], A.subtract, ["nsel", "c10"], ["ownn"])
        for jb in range(3):
            todo = [(T.bob, "bob", b + R * (jb - j2), key) for (j2, b, key) in tiles if j2 < jb] + [(T.thr, "thr", b, key) for (j2, b, key) in tiles if j2 == jb]
            for i in range(len(todo)):
                wm, wk, b, key = todo[i]
                mm(T.ps7[:, 128 + R * jb:128 + R * jb + R], wm[:, :], T.eqb[:, b:b + R], [wk, key], ["B7"], i == 0, i == len(todo) - 1)
        LW = 3 * M
        cp(T.pl[:, 0:LW:M], T.ownn[:, 1:6:2], ["ownn"], ["pl"])
        cp(T.pl[:, 1:LW:M], T.ownn[:, 0:6:2], ["ownn"], ["pl"])
        if M == 4:
            cp(T.pl[:, 2:12:4], T.owno[:, 3:6], ["owno"], ["pl"])
            cp(T.pl[:, 3:12:4], T.owno[:, 0:3], ["owno"], ["pl"])
        if not last:
            act(T.zp[:, 0:16 * LW], Zall.indirect(T.pl[:, 0:LW]), Zk + ["pl"], ["zp"])
        act(T.sp[:, 0:16 * LW], T.S[:, :].indirect(T.pl[:, 0:LW]), Sk + ["pl"], ["sp"])
        for s_ in range(2):
            tt(T.dn[:, s_:LW:M], T.ownn[:, s_:6:2], T.pad8[:, 12 + s_:12 + LW:M], A.subtract, ["ownn", "pad8"], ["dnN"])
        early(last)
        tt(T.cm[:, 0:3 * R], T.ps7[:, 128:128 + 3 * R], T.dm[:, 0:3 * R], A.mult, ["B7", "dm"], ["cm"])
        for jb in range(3):
            red(T.m3[:, jb:jb + 1], T.cm[:, R * jb:R * jb + R], A.max, ["cm"], ["m3"])
        dk = ["dnN", "dnO"] if M == 4 else ["dnN"]
        for jb in range(3):
            ts(T.of1[:, M * jb:M * jb + M], T.dn[:, M * jb:M * jb + M], T.m3[:, jb:jb + 1], A.add, dk + ["m3"], ["of1"], 0.0, A.min)
        tt(T.of2[:, 0:LW], T.of1[:, 0:LW], T.pad8[:, 0:LW], A.add, ["of1", "pad8"], ["of2"])
        cp(T.offs[:, 0:LW], T.of2[:, 0:LW], ["of2"], ["offs"])
        if not last:
            cp(Zall.indirect(T.offs[:, 0:LW]), T.zp[:, 0:16 * LW], ["offs", "zp"], Zk)
        if not last:
            ts(T.hitb[:, :], T.ko[:, :], 19.5, A.is_lt, ["ko"], ["hitb"])
            mm(T.ps7[:, 384:387], T.onb[:, :], T.hitb[:, :], ["onb", "hitb"], ["B7"])
        early(not last)
        for q in range(2):
            ts(T.acc[:, q:6:2], T.m3[:, :], 12288.0, A.is_lt, ["m3"], ["acc"])
        tt(T.ab6[:, :], T.val6[:, :], T.acc[:, 0:6], A.mult, ["val6", "acc"], ["ab6"])
        if last:
            ts(T.ab6[:, :], T.ab6[:, :], -1.0, A.add, ["ab6"], ["ab6"])
        for jb in range(3):
            for a in range(1, 3):
                c = 60 * a + 20 * jb
                ts(T.xs[:, c:c + 20], T.iof[:, 0:20], T.kst[:, jb:jb + 1], A.is_equal, ["iof", "kst", "ab6"], ["xs"], T.ab6[:, 2 * jb + a - 1:2 * jb + a], A.mult)
        if not last:
            sok = "so%d" % t
            tt(T[sok][:, :], T.ts3[:, :], T.xs[:, :], A.add, ["ts3", "xs"], [sok])
            dst, src_ap = nxt, T[sok][:, :]
        else:
            fin_part(1)
            fin_part(2)
            sok = "sf"
            dst, src_ap = prv, T.sf[:, :]
        deps("g", [sok], [])
        rid, pid = topo.addr(dst, core)
        en = topo.engines(core, dst)[:8]
        g.remote_dma(out_ap=T["st%d" % (t + 1)][:, :], in_ap=src_ap, remote_sem=T.sem["arr%d" % (t + 1)], local_sem=T.sem.lsem,
                     pid=pid, routing_id=rid, dma_engine_mask=sum(1 << e for e in en))
        cnt["sent"] = cnt.get("sent", 0) + len(en)
        frm = prv if not last else nxt
        wr["st%d" % (t + 1)] = ("arr%d" % (t + 1), len(topo.engines(frm, core)[:8]), "remote")
        cp(T.S[:, :].indirect(T.offs[:, 0:LW]), T.sp[:, 0:16 * LW], ["offs", "sp"], Sk)
        if last:
            dma("y", T.ys[:, :], T.S[0:128:16, 0:4096], "dout", Sk, [])
            break
        red(T.cc[:, :], T.ps7[:, 384:387], A.add, ["B7"], ["cc"])
        if t == 0:
            cp(T.la[:, :], T.lai[:, :], ["lai"], ["la"])
        yphase(lambda i, t=t: lists(t + 1, i))

    fin = T["st%d" % VI]
    k = "st%d" % VI
    dma("y", T.yk[:, :], fin[:, 0:60], "dout", [k], [])
    dma("s", T.ya[:, :], fin[:, 60:120], "dout", [k], [])
    dma("y", T.yb[:, :], fin[:, 120:180], "dout", [k], [])
    need("y", "dout", 64)
    need("g", "lsem", cnt["sent"])
    for q in ("v", "s", "p", "g"):
        need("g", semn[q], cnt[q])
